import numpy as np
import ml_dtypes


def mxq(x, axis, fmt="e4m3"):
    dtype, down = {"e4m3": (ml_dtypes.float8_e4m3fn, 7), "e5m2": (ml_dtypes.float8_e5m2, 14)}[fmt]
    v = np.moveaxis(np.asarray(x, np.float32).astype(ml_dtypes.bfloat16).astype(np.float64), axis, -1)
    blocks = v.reshape(v.shape[:-1] + (-1, 32))
    amax = np.abs(blocks).max(-1, keepdims=True)
    byte = np.maximum(np.where(amax > 0, np.frexp(amax)[1] - 1 + 127, 0) - down, 1)
    scale = np.exp2(byte - 127.0)
    codes = (blocks / scale).astype(np.float32).astype(dtype).astype(np.float64)
    return np.moveaxis((codes * scale).reshape(v.shape), -1, axis)


WIDE = False


def mx_kscale(k):
    if not WIDE:
        return np.ones(k)
    levels = np.array([10, -10, 5, -5, 0])
    if k % 512:
        return np.exp2(np.random.permutation(np.resize(levels, k // 32))).repeat(32)
    a = np.empty((k // 512, 16))
    for p in range(k // 512):
        a[p, :8] = np.random.permutation(np.resize(levels, 8))
        for g in range(8):
            far = levels[np.abs(levels - a[p, g]) >= 10]
            a[p, g + 8] = far[np.random.randint(len(far))]
    return np.exp2(a.ravel()).repeat(32)


def f64(x):
    return np.asarray(x).astype(np.float64)


def striped(idx):
    return np.tile(np.asarray(idx).reshape(-1, 16).T, (8, 1)).astype(np.uint16)


def unstriped(offs):
    return offs[:16].T.reshape(-1).astype(np.int64)


G, T, D, H = 1024, 2048, 512, 1024


def setup_inputs():
    n = np.random.standard_normal
    s = mx_kscale(D)[:, None]
    u = mx_kscale(H)[:, None]
    return {
        "xT": (n((D, T)) * s).astype(np.float32),
        "w1": (n((D, H)) / np.sqrt(D) / s * u[:, 0]).astype(np.float32),
        "w2": (n((H, D)) / np.sqrt(H) / u * s[:, 0]).astype(np.float32),
        "offs": striped(np.random.permutation(T)[:G]),
    }


def reference(xT, w1, w2, offs):
    x = f64(xT)
    idx = unstriped(offs)
    a = mxq(f64(w1), 0, "e4m3").T @ mxq(x[:, idx], 0, "e4m3")
    h = np.maximum(a, 0.0)
    y = x[:, idx] + (mxq(f64(w2), 0, "e4m3").T @ mxq(h, 0, "e4m3"))
    out = x.copy()
    out[:, idx] = y
    return out

@@ -1,0 +1,208 @@
+from contextlib import ExitStack
+
+import concourse.mybir as mybir
+
+D, T, G, H = 512, 2048, 1024, 1024
+FLOPS = 2 * 2 * D * H * G
+
+F32 = mybir.dt.float32
+BF16 = mybir.dt.bfloat16
+U32 = mybir.dt.uint32
+U16 = mybir.dt.uint16
+U8 = mybir.dt.uint8
+FP8X4 = mybir.dt.float8_e4m3fn_x4
+RELU = mybir.ActivationFunctionType.Relu
+MULT, ADD, MAX = mybir.AluOpType.mult, mybir.AluOpType.add, mybir.AluOpType.max
+
+P = 128
+PACK = 4
+K_PASS = P * PACK
+HALF = 512
+NB = 128
+HIDDEN_PASSES = H // K_PASS
+
+
+def tile_attend_mod_relu_kernel(tc, xT, w1, w2, offs, out):
+    nc = tc.nc
+    with ExitStack() as ctx:
+        keep = ctx.enter_context(tc.tile_pool(name="keep", bufs=1))
+        psum1 = ctx.enter_context(tc.psum_pool(name="psum1", bufs=4))
+        psum2 = ctx.enter_context(tc.psum_pool(name="psum2", bufs=4))
+
+        warm = keep.tile([P, 1], F32, name="warm")
+        nc.vector.memset(warm[:], 0.0)
+        nc.scalar.activation(warm[:], warm[:], RELU)
+
+        offsets = keep.tile([P, G // 16], U16, name="offsets")
+        nc.sync.dma_start(offsets[:], offs)
+        x_rows = xT.rearrange("(p t) c -> t p c", t=PACK)
+        out_rows = out.rearrange("(p t) c -> t p c", t=PACK)
+        w1_rows = w1.rearrange("(p j) c -> p j c", j=PACK)
+        planes = [keep.tile([P, T], F32, name=f"plane{t}") for t in range(PACK)]
+        w1_raw = [keep.tile([P, PACK, K_PASS], F32, name=f"w1_raw{g}") for g in range(HIDDEN_PASSES)]
+        w2_raw = [keep.tile([P, PACK, D], F32, name=f"w2_raw{g}") for g in range(HIDDEN_PASSES)]
+
+        def load_x(t):
+            nc.sync.dma_start(planes[t][:], x_rows[t])
+
+        def load_w1(g):
+            nc.sync.dma_start(w1_raw[g][:], w1_rows[:, :, g * K_PASS : (g + 1) * K_PASS])
+
+        def load_w2(g, c0, c1):
+            rows = w2[g * K_PASS : (g + 1) * K_PASS, :].rearrange("(p j) c -> p j c", j=PACK)
+            nc.sync.dma_start(w2_raw[g][:, :, c0:c1], rows[:, :, c0:c1])
+
+        for t in range(PACK):
+            load_x(t)
+        load_w1(0)
+        load_w1(1)
+        load_w2(0, 0, D)
+        load_w2(1, 0, D // 2)
+        load_w2(1, D // 2, D)
+
+        def group_views(raw, grouped, m0, m1):
+            dst = grouped[:].rearrange("p (t m j) -> p m t j", t=PACK, j=PACK)[:, m0:m1]
+            src = raw[:].rearrange("p j (m t) -> p m t j", t=PACK)[:, m0:m1]
+            return dst, src
+
+        def on_vector(dst, src):
+            nc.vector.tensor_copy(dst, src)
+
+        def on_scalar(dst, src):
+            nc.scalar.copy(dst, src)
+
+        def on_gpsimd(dst, src):
+            nc.gpsimd.tensor_scalar(dst, src, 1.0, 0.0, MULT, ADD)
+
+        def group_weight(raw, label, tag, shares):
+            grouped = keep.tile([P, K_PASS * PACK], BF16, align_bytes=64, tag=tag, name=f"{label}_grouped")
+            for engine, m0, m1 in shares:
+                engine(*group_views(raw, grouped, m0, m1))
+            return grouped
+
+        def quantize(grouped, label):
+            codes = keep.tile([P, K_PASS], U32, align_bytes=64, name=f"{label}_codes")
+            scales = keep.tile([P, K_PASS], U8, align_bytes=64, name=f"{label}_scales")
+            nc.vector.quantize_mx(out=codes[:].bitcast(FP8X4), scales=scales[:], in_=grouped[:])
+            return codes, scales
+
+        def quantize_3d(grouped, label, tag):
+            codes = keep.tile([P, HALF], U32, align_bytes=64, tag=tag, name=f"{label}_codes")
+            scales = keep.tile([P, HALF], U8, align_bytes=64, name=f"{label}_scales")
+            nc.vector.quantize_mx(
+                out=codes[:].bitcast(FP8X4), scales=scales[:], in_=grouped[:].rearrange("p n t -> p (n t)")
+            )
+            return codes, scales
+
+        picked = keep.tile([P, PACK, G], F32, name="picked")
+
+        def gather(t, n0, n1):
+            nc.vector.tensor_copy(picked[:, t, n0:n1], planes[t][:].indirect(offsets[:, n0 // 16 : n1 // 16]))
+
+        def group_x(grouped, h, engine, t0, t1):
+            engine(
+                grouped[:, :, t0:t1],
+                picked[:, t0:t1, h * HALF : (h + 1) * HALF].rearrange("p t n -> p n t"),
+            )
+
+        def first_layer(grouped, x_mx, w_mx, engines):
+            for b in range(HALF // NB):
+                cols = slice(b * NB, (b + 1) * NB)
+                acc = psum1.tile([P, PACK, NB], F32, name="acc1")
+                for t in range(PACK):
+                    chans = slice(t * P, (t + 1) * P)
+                    nc.tensor.matmul_mx(
+                        out=acc[:, t, :],
+                        lhsT=w_mx[0][:, chans].bitcast(FP8X4),
+                        lhsT_scale=w_mx[1][:, chans],
+                        rhs=x_mx[0][:, cols].bitcast(FP8X4),
+                        rhs_scale=x_mx[1][:, cols],
+                        start=True,
+                        stop=True,
+                    )
+                src = acc[:].rearrange("p t n -> p n t")
+                if engines[b] == "v":
+                    nc.vector.tensor_scalar_max(grouped[:, cols, :], src, 0.0)
+                else:
+                    nc.scalar.activation(grouped[:, cols, :], src, RELU)
+
+        def second_layer(t, h_mx):
+            acc = psum2.tile([P, HALF], F32, name="acc2")
+            chans = slice(t * P, (t + 1) * P)
+            for g in range(HIDDEN_PASSES):
+                nc.tensor.matmul_mx(
+                    out=acc[:],
+                    lhsT=w2_mx[g][0][:, chans].bitcast(FP8X4),
+                    lhsT_scale=w2_mx[g][1][:, chans],
+                    rhs=h_mx[g][0][:].bitcast(FP8X4),
+                    rhs_scale=h_mx[g][1][:],
+                    start=(g == 0),
+                    stop=(g == HIDDEN_PASSES - 1),
+                )
+            return acc
+
+        def add(h, t, acc, tag):
+            y = keep.tile([P, HALF], F32, align_bytes=64, tag=tag, name=f"y{h}{t}")
+            nc.vector.tensor_tensor(y[:], acc[:], picked[:, t, h * HALF : (h + 1) * HALF], ADD)
+            return y
+
+        def add_apart(h, t, acc, tag):
+            product = keep.tile([P, HALF], F32, name=f"product{h}{t}")
+            nc.scalar.copy(product[:], acc[:])
+            y = keep.tile([P, HALF], F32, align_bytes=64, tag=tag, name=f"y{h}{t}")
+            nc.gpsimd.tensor_tensor(y[:], product[:], picked[:, t, h * HALF : (h + 1) * HALF], ADD)
+            return y
+
+        def scatter(h, t, y):
+            nc.vector.tensor_copy(planes[t][:].indirect(offsets[:, h * HALF // 16 : (h + 1) * HALF // 16]), y[:])
+
+        for t in range(PACK - 1):
+            gather(t, 0, G)
+        gather(PACK - 1, 0, HALF)
+        gather(PACK - 1, HALF, G)
+        xa = keep.tile([P, HALF, PACK], BF16, align_bytes=64, tag="slot_a", name="xa_grouped")
+        xb = keep.tile([P, HALF, PACK], BF16, align_bytes=64, name="xb_grouped")
+        group_x(xa, 0, on_scalar, 0, 2)
+        group_x(xb, 1, on_scalar, 0, 2)
+        group_x(xa, 0, on_scalar, 2, 4)
+        w1a = group_weight(w1_raw[0], "w1a", "slot_b", [(on_gpsimd, 0, 96), (on_vector, 96, P)])
+        xa_mx = quantize_3d(xa, "xa", "x_codes")
+        w1_mx = [quantize(w1a, "w1a")]
+        group_x(xb, 1, on_scalar, 2, 4)
+        ha0 = keep.tile([P, HALF, PACK], BF16, align_bytes=64, name="ha0_grouped")
+        first_layer(ha0, xa_mx, w1_mx[0], "ssss")
+        w1b = group_weight(w1_raw[1], "w1b", "slot_a", [(on_gpsimd, 0, 96), (on_vector, 96, P)])
+        w1_mx.append(quantize(w1b, "w1b"))
+        ha1 = keep.tile([P, HALF, PACK], BF16, align_bytes=64, name="ha1_grouped")
+        first_layer(ha1, xa_mx, w1_mx[1], "ssss")
+        ha_mx = [quantize_3d(ha0, "ha0", "ha0_codes")]
+        xb_mx = quantize_3d(xb, "xb", "x_codes")
+        w2a = group_weight(w2_raw[0], "w2a", "slot_b", [(on_gpsimd, 0, 96), (on_vector, 96, P)])
+        w2_mx = [quantize(w2a, "w2a")]
+        w2b = group_weight(w2_raw[1], "w2b", "slot_a", [(on_gpsimd, 0, 64), (on_vector, 64, P)])
+        ha_mx.append(quantize_3d(ha1, "ha1", "ha1_codes"))
+        w2_mx.append(quantize(w2b, "w2b"))
+        acc_a = [second_layer(t, ha_mx) for t in range(PACK)]
+        y0 = add(0, 0, acc_a[0], "y00")
+        y1 = add_apart(0, 1, acc_a[1], "y01")
+        scatter(0, 0, y0)
+        hb = keep.tile([P, HIDDEN_PASSES, HALF, PACK], BF16, align_bytes=64, tag="slot_e", name="hb_grouped")
+        first_layer(hb[:, 0], xb_mx, w1_mx[0], "ssss")
+        y2 = add_apart(0, 2, acc_a[2], "y02")
+        first_layer(hb[:, 1], xb_mx, w1_mx[1], "ssss")
+        scatter(0, 1, y1)
+        hb_codes = keep.tile([P, HIDDEN_PASSES, HALF], U32, align_bytes=64, name="hb_codes")
+        hb_scales = keep.tile([P, HIDDEN_PASSES, HALF], U8, align_bytes=64, name="hb_scales")
+        nc.vector.quantize_mx(
+            out=hb_codes[:].rearrange("p g n -> p (g n)").bitcast(FP8X4),
+            scales=hb_scales[:].rearrange("p g n -> p (g n)"),
+            in_=hb[:].rearrange("p g n t -> p (g n t)"),
+        )
+        hb_mx = [(hb_codes[:, g], hb_scales[:, g]) for g in range(HIDDEN_PASSES)]
+        scatter(0, 2, y2)
+        y3 = add(0, 3, acc_a[3], "slot_e")
+        scatter(0, 3, y3)
+        for t in range(PACK):
+            y_b = add_apart(1, t, second_layer(t, hb_mx), f"y1{t}")
+            scatter(1, t, y_b)
+            nc.sync.dma_start(out_rows[t], planes[t][:])

@@ -12,103 +12,88 @@ U16 = mybir.dt.uint16
 U8 = mybir.dt.uint8
 FP8X4 = mybir.dt.float8_e4m3fn_x4
 RELU = mybir.ActivationFunctionType.Relu
-MULT, ADD, MAX = mybir.AluOpType.mult, mybir.AluOpType.add, mybir.AluOpType.max
+ADD = mybir.AluOpType.add
 
 P = 128
 PACK = 4
 K_PASS = P * PACK
 HALF = 512
+QUARTER = 256
 NB = 128
 HIDDEN_PASSES = H // K_PASS
+BANKS = 4
 
 
 def tile_attend_mod_relu_kernel(tc, xT, w1, w2, offs, out):
     nc = tc.nc
     with ExitStack() as ctx:
         keep = ctx.enter_context(tc.tile_pool(name="keep", bufs=1))
-        psum1 = ctx.enter_context(tc.psum_pool(name="psum1", bufs=4))
-        psum2 = ctx.enter_context(tc.psum_pool(name="psum2", bufs=4))
+        psum = ctx.enter_context(tc.psum_pool(name="psum", bufs=1))
 
-        warm = keep.tile([P, 1], F32, name="warm")
-        nc.vector.memset(warm[:], 0.0)
-        nc.scalar.activation(warm[:], warm[:], RELU)
+        def sbuf(shape, dtype, label, tag=None):
+            return keep.tile(shape, dtype, align_bytes=64, tag=tag or label, name=label)
 
         offsets = keep.tile([P, G // 16], U16, name="offsets")
         nc.sync.dma_start(offsets[:], offs)
         x_rows = xT.rearrange("(p t) c -> t p c", t=PACK)
         out_rows = out.rearrange("(p t) c -> t p c", t=PACK)
         w1_rows = w1.rearrange("(p j) c -> p j c", j=PACK)
-        planes = [keep.tile([P, T], F32, name=f"plane{t}") for t in range(PACK)]
-        w1_raw = [keep.tile([P, PACK, K_PASS], F32, name=f"w1_raw{g}") for g in range(HIDDEN_PASSES)]
-        w2_raw = [keep.tile([P, PACK, D], F32, name=f"w2_raw{g}") for g in range(HIDDEN_PASSES)]
-
-        def load_x(t):
-            nc.sync.dma_start(planes[t][:], x_rows[t])
-
-        def load_w1(g):
-            nc.sync.dma_start(w1_raw[g][:], w1_rows[:, :, g * K_PASS : (g + 1) * K_PASS])
-
-        def load_w2(g, c0, c1):
-            rows = w2[g * K_PASS : (g + 1) * K_PASS, :].rearrange("(p j) c -> p j c", j=PACK)
-            nc.sync.dma_start(w2_raw[g][:, :, c0:c1], rows[:, :, c0:c1])
+        planes = [sbuf([P, T], F32, f"plane{t}") for t in range(PACK)]
+        w1_raw = [sbuf([P, PACK, K_PASS], F32, f"w1_raw{g}") for g in range(HIDDEN_PASSES)]
+        w2_raw = [sbuf([P, PACK, D], F32, f"w2_raw{g}") for g in range(HIDDEN_PASSES)]
 
         for t in range(PACK):
-            load_x(t)
-        load_w1(0)
-        load_w1(1)
-        load_w2(0, 0, D)
-        load_w2(1, 0, D // 2)
-        load_w2(1, D // 2, D)
+            nc.sync.dma_start(planes[t][:], x_rows[t])
+        for g in range(HIDDEN_PASSES):
+            nc.sync.dma_start(w1_raw[g][:], w1_rows[:, :, g * K_PASS : (g + 1) * K_PASS])
+        for g in range(HIDDEN_PASSES):
+            rows = w2[g * K_PASS : (g + 1) * K_PASS, :].rearrange("(p j) c -> p j c", j=PACK)
+            nc.sync.dma_start(w2_raw[g][:], rows)
 
-        def group_views(raw, grouped, m0, m1):
-            dst = grouped[:].rearrange("p (t m j) -> p m t j", t=PACK, j=PACK)[:, m0:m1]
-            src = raw[:].rearrange("p j (m t) -> p m t j", t=PACK)[:, m0:m1]
-            return dst, src
+        def group_weight(raw, label, split):
+            grouped = sbuf([P, K_PASS * PACK], BF16, label)
+            dst = grouped[:].rearrange("p (t m j) -> p m j t", t=PACK, j=PACK)
+            src = raw[:].rearrange("p j (m t) -> p m j t", t=PACK)
+            nc.vector.tensor_copy(dst[:, :split], src[:, :split])
+            if split < P:
+                nc.scalar.copy(dst[:, split:], src[:, split:])
+            return grouped[:]
 
-        def on_vector(dst, src):
-            nc.vector.tensor_copy(dst, src)
+        def mx_tiles(width, label, tag=None):
+            return sbuf([P, width], U32, f"{label}_codes", tag), sbuf([P, width], U8, f"{label}_scales")
 
-        def on_scalar(dst, src):
-            nc.scalar.copy(dst, src)
-
-        def on_gpsimd(dst, src):
-            nc.gpsimd.tensor_scalar(dst, src, 1.0, 0.0, MULT, ADD)
-
-        def group_weight(raw, label, tag, shares):
-            grouped = keep.tile([P, K_PASS * PACK], BF16, align_bytes=64, tag=tag, name=f"{label}_grouped")
-            for engine, m0, m1 in shares:
-                engine(*group_views(raw, grouped, m0, m1))
-            return grouped
-
-        def quantize(grouped, label):
-            codes = keep.tile([P, K_PASS], U32, align_bytes=64, name=f"{label}_codes")
-            scales = keep.tile([P, K_PASS], U8, align_bytes=64, name=f"{label}_scales")
-            nc.vector.quantize_mx(out=codes[:].bitcast(FP8X4), scales=scales[:], in_=grouped[:])
-            return codes, scales
-
-        def quantize_3d(grouped, label, tag):
-            codes = keep.tile([P, HALF], U32, align_bytes=64, tag=tag, name=f"{label}_codes")
-            scales = keep.tile([P, HALF], U8, align_bytes=64, name=f"{label}_scales")
+        def quantize(mx, grouped, c0, c1):
             nc.vector.quantize_mx(
-                out=codes[:].bitcast(FP8X4), scales=scales[:], in_=grouped[:].rearrange("p n t -> p (n t)")
+                out=mx[0][:, c0:c1].bitcast(FP8X4), scales=mx[1][:, c0:c1], in_=grouped[:, c0 * PACK : c1 * PACK]
             )
-            return codes, scales
 
-        picked = keep.tile([P, PACK, G], F32, name="picked")
+        def quantized(grouped, label, tag=None):
+            width = grouped.shape[1] // PACK
+            mx = mx_tiles(width, label, tag)
+            quantize(mx, grouped, 0, width)
+            return mx
+
+        picked = sbuf([P, PACK, G], F32, "picked")
+
+        def listed(t, n0, n1):
+            return planes[t][:].indirect(offsets[:, n0 // 16 : n1 // 16])
 
         def gather(t, n0, n1):
-            nc.vector.tensor_copy(picked[:, t, n0:n1], planes[t][:].indirect(offsets[:, n0 // 16 : n1 // 16]))
+            nc.vector.tensor_copy(picked[:, t, n0:n1], listed(t, n0, n1))
 
-        def group_x(grouped, h, engine, t0, t1):
-            engine(
-                grouped[:, :, t0:t1],
-                picked[:, t0:t1, h * HALF : (h + 1) * HALF].rearrange("p t n -> p n t"),
-            )
+        def group_x(grouped, n0, n1, t0, t1):
+            dst = grouped[:].rearrange("p (n t) -> p n t", t=PACK)
+            nc.scalar.copy(dst[:, :, t0:t1], picked[:, t0:t1, n0:n1].rearrange("p t n -> p n t"))
 
-        def first_layer(grouped, x_mx, w_mx, engines):
-            for b in range(HALF // NB):
-                cols = slice(b * NB, (b + 1) * NB)
-                acc = psum1.tile([P, PACK, NB], F32, name="acc1")
+        first_banks = []
+        second_banks = []
+
+        def first_layer(grouped, x_mx, c0, w_mx):
+            dst = grouped.rearrange("p (n t) -> p n t", t=PACK)
+            for b in range(dst.shape[1] // NB):
+                cols = slice(c0 + b * NB, c0 + (b + 1) * NB)
+                acc = psum.tile([P, PACK, NB], F32, tag=f"first{len(first_banks) % BANKS}", name="acc1")
+                first_banks.append(acc)
                 for t in range(PACK):
                     chans = slice(t * P, (t + 1) * P)
                     nc.tensor.matmul_mx(
@@ -120,89 +105,80 @@ def tile_attend_mod_relu_kernel(tc, xT, w1, w2, offs, out):
                         start=True,
                         stop=True,
                     )
-                src = acc[:].rearrange("p t n -> p n t")
-                if engines[b] == "v":
-                    nc.vector.tensor_scalar_max(grouped[:, cols, :], src, 0.0)
-                else:
-                    nc.scalar.activation(grouped[:, cols, :], src, RELU)
+                nc.scalar.activation(dst[:, b * NB : (b + 1) * NB, :], acc[:].rearrange("p t n -> p n t"), RELU)
 
-        def second_layer(t, h_mx):
-            acc = psum2.tile([P, HALF], F32, name="acc2")
-            chans = slice(t * P, (t + 1) * P)
-            for g in range(HIDDEN_PASSES):
-                nc.tensor.matmul_mx(
-                    out=acc[:],
-                    lhsT=w2_mx[g][0][:, chans].bitcast(FP8X4),
-                    lhsT_scale=w2_mx[g][1][:, chans],
-                    rhs=h_mx[g][0][:].bitcast(FP8X4),
-                    rhs_scale=h_mx[g][1][:],
-                    start=(g == 0),
-                    stop=(g == HIDDEN_PASSES - 1),
-                )
-            return acc
-
-        def add(h, t, acc, tag):
-            y = keep.tile([P, HALF], F32, align_bytes=64, tag=tag, name=f"y{h}{t}")
-            nc.vector.tensor_tensor(y[:], acc[:], picked[:, t, h * HALF : (h + 1) * HALF], ADD)
-            return y
-
-        def add_apart(h, t, acc, tag):
-            product = keep.tile([P, HALF], F32, name=f"product{h}{t}")
+        def second_layer(ts, width, h_cols, w_mx, label, after_first=False):
+            if after_first:
+                bank = f"first{(len(first_banks) - 1) % BANKS}"
+            else:
+                bank = f"second{len(second_banks) % BANKS}"
+                second_banks.append(bank)
+            acc = psum.tile([P, len(ts), width], F32, tag=bank, name="acc2")
+            for k, t in enumerate(ts):
+                chans = slice(t * P, (t + 1) * P)
+                for g in range(HIDDEN_PASSES):
+                    codes, scales, c0 = h_cols[g]
+                    nc.tensor.matmul_mx(
+                        out=acc[:, k, :],
+                        lhsT=w_mx[g][0][:, chans].bitcast(FP8X4),
+                        lhsT_scale=w_mx[g][1][:, chans],
+                        rhs=codes[:, c0 : c0 + width].bitcast(FP8X4),
+                        rhs_scale=scales[:, c0 : c0 + width],
+                        start=(g == 0),
+                        stop=(g == HIDDEN_PASSES - 1),
+                    )
+            product = sbuf([P, len(ts), width], F32, label)
             nc.scalar.copy(product[:], acc[:])
-            y = keep.tile([P, HALF], F32, align_bytes=64, tag=tag, name=f"y{h}{t}")
-            nc.gpsimd.tensor_tensor(y[:], product[:], picked[:, t, h * HALF : (h + 1) * HALF], ADD)
-            return y
+            return product
 
-        def scatter(h, t, y):
-            nc.vector.tensor_copy(planes[t][:].indirect(offsets[:, h * HALF // 16 : (h + 1) * HALF // 16]), y[:])
+        def scatter(ts, n0, n1, product):
+            for k, t in enumerate(ts):
+                nc.vector.tensor_tensor(listed(t, n0, n1), product[:, k, :], picked[:, t, n0:n1], ADD)
 
         for t in range(PACK - 1):
             gather(t, 0, G)
         gather(PACK - 1, 0, HALF)
         gather(PACK - 1, HALF, G)
-        xa = keep.tile([P, HALF, PACK], BF16, align_bytes=64, tag="slot_a", name="xa_grouped")
-        xb = keep.tile([P, HALF, PACK], BF16, align_bytes=64, name="xb_grouped")
-        group_x(xa, 0, on_scalar, 0, 2)
-        group_x(xb, 1, on_scalar, 0, 2)
-        group_x(xa, 0, on_scalar, 2, 4)
-        w1a = group_weight(w1_raw[0], "w1a", "slot_b", [(on_gpsimd, 0, 96), (on_vector, 96, P)])
-        xa_mx = quantize_3d(xa, "xa", "x_codes")
-        w1_mx = [quantize(w1a, "w1a")]
-        group_x(xb, 1, on_scalar, 2, 4)
-        ha0 = keep.tile([P, HALF, PACK], BF16, align_bytes=64, name="ha0_grouped")
-        first_layer(ha0, xa_mx, w1_mx[0], "ssss")
-        w1b = group_weight(w1_raw[1], "w1b", "slot_a", [(on_gpsimd, 0, 96), (on_vector, 96, P)])
-        w1_mx.append(quantize(w1b, "w1b"))
-        ha1 = keep.tile([P, HALF, PACK], BF16, align_bytes=64, name="ha1_grouped")
-        first_layer(ha1, xa_mx, w1_mx[1], "ssss")
-        ha_mx = [quantize_3d(ha0, "ha0", "ha0_codes")]
-        xb_mx = quantize_3d(xb, "xb", "x_codes")
-        w2a = group_weight(w2_raw[0], "w2a", "slot_b", [(on_gpsimd, 0, 96), (on_vector, 96, P)])
-        w2_mx = [quantize(w2a, "w2a")]
-        w2b = group_weight(w2_raw[1], "w2b", "slot_a", [(on_gpsimd, 0, 64), (on_vector, 64, P)])
-        ha_mx.append(quantize_3d(ha1, "ha1", "ha1_codes"))
-        w2_mx.append(quantize(w2b, "w2b"))
-        acc_a = [second_layer(t, ha_mx) for t in range(PACK)]
-        y0 = add(0, 0, acc_a[0], "y00")
-        y1 = add_apart(0, 1, acc_a[1], "y01")
-        scatter(0, 0, y0)
-        hb = keep.tile([P, HIDDEN_PASSES, HALF, PACK], BF16, align_bytes=64, tag="slot_e", name="hb_grouped")
-        first_layer(hb[:, 0], xb_mx, w1_mx[0], "ssss")
-        y2 = add_apart(0, 2, acc_a[2], "y02")
-        first_layer(hb[:, 1], xb_mx, w1_mx[1], "ssss")
-        scatter(0, 1, y1)
-        hb_codes = keep.tile([P, HIDDEN_PASSES, HALF], U32, align_bytes=64, name="hb_codes")
-        hb_scales = keep.tile([P, HIDDEN_PASSES, HALF], U8, align_bytes=64, name="hb_scales")
-        nc.vector.quantize_mx(
-            out=hb_codes[:].rearrange("p g n -> p (g n)").bitcast(FP8X4),
-            scales=hb_scales[:].rearrange("p g n -> p (g n)"),
-            in_=hb[:].rearrange("p g n t -> p (g n t)"),
-        )
-        hb_mx = [(hb_codes[:, g], hb_scales[:, g]) for g in range(HIDDEN_PASSES)]
-        scatter(0, 2, y2)
-        y3 = add(0, 3, acc_a[3], "slot_e")
-        scatter(0, 3, y3)
+        xa = sbuf([P, HALF * PACK], BF16, "xa")
+        xb = sbuf([P, HALF * PACK], BF16, "xb")
+        group_x(xa, 0, HALF, 0, 2)
+        group_x(xb, HALF, G, 0, 2)
+        group_x(xa, 0, HALF, 2, 4)
+        group_x(xb, HALF, G, 2, 4)
+        w1a = group_weight(w1_raw[0], "w1a", P)
+        xa_mx = quantized(xa[:], "xa", "w1_raw0")
+        w1_mx = [quantized(w1a, "w1a")]
+        w1b = group_weight(w1_raw[1], "w1b", 80)
+        ha = [sbuf([P, QUARTER * PACK], BF16, f"ha{g}") for g in range(HIDDEN_PASSES)]
+        first_layer(ha[0][:], xa_mx, 0, w1_mx[0])
+        xb_mx = quantized(xb[:], "xb", "w1_raw1")
+        w1_mx.append(quantized(w1b, "w1b"))
+        w2a = group_weight(w2_raw[0], "w2a", 84)
+        first_layer(ha[1][:], xa_mx, 0, w1_mx[1])
+        ha_mx = [quantized(ha[0][:], "ha0")]
+        w2_mx = [quantized(w2a, "w2a")]
+        w2b = group_weight(w2_raw[1], "w2b", 88)
+        ha_mx.append(quantized(ha[1][:], "ha1"))
+        w2_mx.append(mx_tiles(K_PASS, "w2b"))
+        quantize(w2_mx[1], w2b, 0, P)
+        quantize(w2_mx[1], w2b, P, 2 * P)
+        quantize(w2_mx[1], w2b, 2 * P, K_PASS)
+        ha_cols = [(codes, scales, 0) for codes, scales in ha_mx]
+        for t in range(2):
+            scatter([t], 0, QUARTER, second_layer([t], QUARTER, ha_cols, w2_mx, f"ya{t}"))
+        hb = sbuf([P, HIDDEN_PASSES * QUARTER * PACK], BF16, "hb", "w2_raw1")
+        for g in range(HIDDEN_PASSES):
+            first_layer(hb[:, g * QUARTER * PACK : (g + 1) * QUARTER * PACK], xa_mx, QUARTER, w1_mx[g])
+        hb_mx = quantized(hb[:], "hb")
+        hb_cols = [(hb_mx[0], hb_mx[1], g * QUARTER) for g in range(HIDDEN_PASSES)]
+        scatter([2, 3], 0, QUARTER, second_layer([2, 3], QUARTER, ha_cols, w2_mx, "ya23", True))
+        scatter([0, 1], QUARTER, HALF, second_layer([0, 1], QUARTER, hb_cols, w2_mx, "yb01"))
+        hc = sbuf([P, HIDDEN_PASSES * HALF * PACK], BF16, "hc", "w2b")
+        for g in range(HIDDEN_PASSES):
+            first_layer(hc[:, g * HALF * PACK : (g + 1) * HALF * PACK], xb_mx, 0, w1_mx[g])
+        hc_mx = quantized(hc[:], "hc")
+        hc_cols = [(hc_mx[0], hc_mx[1], g * HALF) for g in range(HIDDEN_PASSES)]
+        scatter([2, 3], QUARTER, HALF, second_layer([2, 3], QUARTER, hb_cols, w2_mx, "yb23", True))
         for t in range(PACK):
-            y_b = add_apart(1, t, second_layer(t, hb_mx), f"y1{t}")
-            scatter(1, t, y_b)
+            scatter([t], HALF, G, second_layer([t], HALF, hc_cols, w2_mx, f"yc{t}"))
             nc.sync.dma_start(out_rows[t], planes[t][:])

@@ -34,7 +34,6 @@ def tile_attend_mod_relu_kernel(tc, xT, w1, w2, offs, out):
             return keep.tile(shape, dtype, align_bytes=64, tag=tag or label, name=label)
 
         offsets = keep.tile([P, G // 16], U16, name="offsets")
-        nc.sync.dma_start(offsets[:], offs)
         x_rows = xT.rearrange("(p t) c -> t p c", t=PACK)
         out_rows = out.rearrange("(p t) c -> t p c", t=PACK)
         w1_rows = w1.rearrange("(p j) c -> p j c", j=PACK)
@@ -42,7 +41,9 @@ def tile_attend_mod_relu_kernel(tc, xT, w1, w2, offs, out):
         w1_raw = [sbuf([P, PACK, K_PASS], F32, f"w1_raw{g}") for g in range(HIDDEN_PASSES)]
         w2_raw = [sbuf([P, PACK, D], F32, f"w2_raw{g}") for g in range(HIDDEN_PASSES)]
 
-        for t in range(PACK):
+        nc.sync.dma_start(planes[0][:], x_rows[0])
+        nc.sync.dma_start(offsets[:], offs)
+        for t in range(1, PACK):
             nc.sync.dma_start(planes[t][:], x_rows[t])
         for g in range(HIDDEN_PASSES):
             nc.sync.dma_start(w1_raw[g][:], w1_rows[:, :, g * K_PASS : (g + 1) * K_PASS])
@@ -54,7 +55,8 @@ def tile_attend_mod_relu_kernel(tc, xT, w1, w2, offs, out):
             grouped = sbuf([P, K_PASS * PACK], BF16, label)
             dst = grouped[:].rearrange("p (t m j) -> p m j t", t=PACK, j=PACK)
             src = raw[:].rearrange("p j (m t) -> p m j t", t=PACK)
-            nc.vector.tensor_copy(dst[:, :split], src[:, :split])
+            if split > 0:
+                nc.vector.tensor_copy(dst[:, :split], src[:, :split])
             if split < P:
                 nc.scalar.copy(dst[:, split:], src[:, split:])
             return grouped[:]
@@ -82,8 +84,8 @@ def tile_attend_mod_relu_kernel(tc, xT, w1, w2, offs, out):
             nc.vector.tensor_copy(picked[:, t, n0:n1], listed(t, n0, n1))
 
         def group_x(grouped, n0, n1, t0, t1):
-            dst = grouped[:].rearrange("p (n t) -> p n t", t=PACK)
-            nc.scalar.copy(dst[:, :, t0:t1], picked[:, t0:t1, n0:n1].rearrange("p t n -> p n t"))
+            dst = grouped.rearrange("p (c i t) -> p c t i", i=PACK, t=PACK)
+            nc.scalar.copy(dst[:, :, t0:t1], picked[:, t0:t1, n0:n1].rearrange("p t (c i) -> p c t i", i=PACK))
 
         first_banks = []
         second_banks = []
@@ -141,23 +143,23 @@ def tile_attend_mod_relu_kernel(tc, xT, w1, w2, offs, out):
         gather(PACK - 1, HALF, G)
         xa = sbuf([P, HALF * PACK], BF16, "xa")
         xb = sbuf([P, HALF * PACK], BF16, "xb")
-        group_x(xa, 0, HALF, 0, 2)
-        group_x(xb, HALF, G, 0, 2)
-        group_x(xa, 0, HALF, 2, 4)
-        group_x(xb, HALF, G, 2, 4)
-        w1a = group_weight(w1_raw[0], "w1a", P)
+        group_x(xa[:], 0, HALF, 0, 2)
+        group_x(xb[:], HALF, G, 0, 2)
+        group_x(xa[:], 0, HALF, 2, 4)
+        group_x(xb[:], HALF, G, 2, 4)
+        w1a = group_weight(w1_raw[0], "w1a", 128)
         xa_mx = quantized(xa[:], "xa", "w1_raw0")
         w1_mx = [quantized(w1a, "w1a")]
-        w1b = group_weight(w1_raw[1], "w1b", 80)
+        xb_mx = quantized(xb[:], "xb", "w1a")
+        w1b = group_weight(w1_raw[1], "w1b", 40)
         ha = [sbuf([P, QUARTER * PACK], BF16, f"ha{g}") for g in range(HIDDEN_PASSES)]
         first_layer(ha[0][:], xa_mx, 0, w1_mx[0])
-        xb_mx = quantized(xb[:], "xb", "w1_raw1")
+        w2a = group_weight(w2_raw[0], "w2a", 128)
         w1_mx.append(quantized(w1b, "w1b"))
-        w2a = group_weight(w2_raw[0], "w2a", 84)
         first_layer(ha[1][:], xa_mx, 0, w1_mx[1])
-        ha_mx = [quantized(ha[0][:], "ha0")]
         w2_mx = [quantized(w2a, "w2a")]
-        w2b = group_weight(w2_raw[1], "w2b", 88)
+        ha_mx = [quantized(ha[0][:], "ha0")]
+        w2b = group_weight(w2_raw[1], "w2b", 128)
         ha_mx.append(quantized(ha[1][:], "ha1"))
         w2_mx.append(mx_tiles(K_PASS, "w2b"))
         quantize(w2_mx[1], w2b, 0, P)
@@ -166,14 +168,14 @@ def tile_attend_mod_relu_kernel(tc, xT, w1, w2, offs, out):
         ha_cols = [(codes, scales, 0) for codes, scales in ha_mx]
         for t in range(2):
             scatter([t], 0, QUARTER, second_layer([t], QUARTER, ha_cols, w2_mx, f"ya{t}"))
-        hb = sbuf([P, HIDDEN_PASSES * QUARTER * PACK], BF16, "hb", "w2_raw1")
+        hb = [sbuf([P, QUARTER * PACK], BF16, f"hb{g}") for g in range(HIDDEN_PASSES)]
+        hb_cols = []
         for g in range(HIDDEN_PASSES):
-            first_layer(hb[:, g * QUARTER * PACK : (g + 1) * QUARTER * PACK], xa_mx, QUARTER, w1_mx[g])
-        hb_mx = quantized(hb[:], "hb")
-        hb_cols = [(hb_mx[0], hb_mx[1], g * QUARTER) for g in range(HIDDEN_PASSES)]
+            first_layer(hb[g][:], xa_mx, QUARTER, w1_mx[g])
+            hb_cols.append((*quantized(hb[g][:], f"hb{g}"), 0))
         scatter([2, 3], 0, QUARTER, second_layer([2, 3], QUARTER, ha_cols, w2_mx, "ya23", True))
         scatter([0, 1], QUARTER, HALF, second_layer([0, 1], QUARTER, hb_cols, w2_mx, "yb01"))
-        hc = sbuf([P, HIDDEN_PASSES * HALF * PACK], BF16, "hc", "w2b")
+        hc = sbuf([P, HIDDEN_PASSES * HALF * PACK], BF16, "hc")
         for g in range(HIDDEN_PASSES):
             first_layer(hc[:, g * HALF * PACK : (g + 1) * HALF * PACK], xb_mx, 0, w1_mx[g])
         hc_mx = quantized(hc[:], "hc")

@@ -21,7 +21,6 @@ HALF = 512
 QUARTER = 256
 NB = 128
 HIDDEN_PASSES = H // K_PASS
-BANKS = 4
 
 
 def tile_attend_mod_relu_kernel(tc, xT, w1, w2, offs, out):
@@ -61,6 +60,10 @@ def tile_attend_mod_relu_kernel(tc, xT, w1, w2, offs, out):
                 nc.scalar.copy(dst[:, split:], src[:, split:])
             return grouped[:]
 
+        def group_planes(grouped, raw, t0, t1, engine):
+            dst = grouped.rearrange("p (t m j) -> p m j t", m=P, j=PACK)
+            engine(dst, raw[:].rearrange("p j (m t) -> p m j t", t=PACK)[:, :, :, t0:t1])
+
         def mx_tiles(width, label, tag=None):
             return sbuf([P, width], U32, f"{label}_codes", tag), sbuf([P, width], U8, f"{label}_scales")
 
@@ -87,15 +90,11 @@ def tile_attend_mod_relu_kernel(tc, xT, w1, w2, offs, out):
             dst = grouped.rearrange("p (c i t) -> p c t i", i=PACK, t=PACK)
             nc.scalar.copy(dst[:, :, t0:t1], picked[:, t0:t1, n0:n1].rearrange("p t (c i) -> p c t i", i=PACK))
 
-        first_banks = []
-        second_banks = []
-
-        def first_layer(grouped, x_mx, c0, w_mx):
+        def first_layer(grouped, x_mx, c0, w_mx, banks):
             dst = grouped.rearrange("p (n t) -> p n t", t=PACK)
             for b in range(dst.shape[1] // NB):
                 cols = slice(c0 + b * NB, c0 + (b + 1) * NB)
-                acc = psum.tile([P, PACK, NB], F32, tag=f"first{len(first_banks) % BANKS}", name="acc1")
-                first_banks.append(acc)
+                acc = psum.tile([P, PACK, NB], F32, tag=f"bank{banks[b]}", name="acc1")
                 for t in range(PACK):
                     chans = slice(t * P, (t + 1) * P)
                     nc.tensor.matmul_mx(
@@ -109,33 +108,31 @@ def tile_attend_mod_relu_kernel(tc, xT, w1, w2, offs, out):
                     )
                 nc.scalar.activation(dst[:, b * NB : (b + 1) * NB, :], acc[:].rearrange("p t n -> p n t"), RELU)
 
-        def second_layer(ts, width, h_cols, w_mx, label, after_first=False):
-            if after_first:
-                bank = f"first{(len(first_banks) - 1) % BANKS}"
-            else:
-                bank = f"second{len(second_banks) % BANKS}"
-                second_banks.append(bank)
-            acc = psum.tile([P, len(ts), width], F32, tag=bank, name="acc2")
-            for k, t in enumerate(ts):
-                chans = slice(t * P, (t + 1) * P)
+        def second_sums(parts, width, w_mx, bank):
+            acc = psum.tile([P, len(parts), width], F32, tag=f"bank{bank}", name="acc2")
+            for k, (t, h_cols) in enumerate(parts):
+                chans = slice(t % 2 * P, (t % 2 + 1) * P)
                 for g in range(HIDDEN_PASSES):
                     codes, scales, c0 = h_cols[g]
                     nc.tensor.matmul_mx(
                         out=acc[:, k, :],
-                        lhsT=w_mx[g][0][:, chans].bitcast(FP8X4),
-                        lhsT_scale=w_mx[g][1][:, chans],
+                        lhsT=w_mx[t // 2][g][0][:, chans].bitcast(FP8X4),
+                        lhsT_scale=w_mx[t // 2][g][1][:, chans],
                         rhs=codes[:, c0 : c0 + width].bitcast(FP8X4),
                         rhs_scale=scales[:, c0 : c0 + width],
                         start=(g == 0),
                         stop=(g == HIDDEN_PASSES - 1),
                     )
-            product = sbuf([P, len(ts), width], F32, label)
+            return acc
+
+        def second_layer(parts, width, w_mx, label, bank, tag=None):
+            acc = second_sums(parts, width, w_mx, bank)
+            product = sbuf([P, len(parts), width], F32, label, tag)
             nc.scalar.copy(product[:], acc[:])
             return product
 
-        def scatter(ts, n0, n1, product):
-            for k, t in enumerate(ts):
-                nc.vector.tensor_tensor(listed(t, n0, n1), product[:, k, :], picked[:, t, n0:n1], ADD)
+        def scatter(t, n0, n1, product):
+            nc.vector.tensor_tensor(listed(t, n0, n1), product, picked[:, t, n0:n1], ADD)
 
         for t in range(PACK - 1):
             gather(t, 0, G)
@@ -147,40 +144,48 @@ def tile_attend_mod_relu_kernel(tc, xT, w1, w2, offs, out):
         group_x(xb[:], HALF, G, 0, 2)
         group_x(xa[:], 0, HALF, 2, 4)
         group_x(xb[:], HALF, G, 2, 4)
-        w1a = group_weight(w1_raw[0], "w1a", 128)
+        w1a = group_weight(w1_raw[0], "w1a", P)
         xa_mx = quantized(xa[:], "xa", "w1_raw0")
         w1_mx = [quantized(w1a, "w1a")]
         xb_mx = quantized(xb[:], "xb", "w1a")
-        w1b = group_weight(w1_raw[1], "w1b", 40)
+        w1b = group_weight(w1_raw[1], "w1b", 64)
         ha = [sbuf([P, QUARTER * PACK], BF16, f"ha{g}") for g in range(HIDDEN_PASSES)]
-        first_layer(ha[0][:], xa_mx, 0, w1_mx[0])
-        w2a = group_weight(w2_raw[0], "w2a", 128)
+        first_layer(ha[0][:], xa_mx, 0, w1_mx[0], (0, 1))
         w1_mx.append(quantized(w1b, "w1b"))
-        first_layer(ha[1][:], xa_mx, 0, w1_mx[1])
-        w2_mx = [quantized(w2a, "w2a")]
-        ha_mx = [quantized(ha[0][:], "ha0")]
-        w2b = group_weight(w2_raw[1], "w2b", 128)
-        ha_mx.append(quantized(ha[1][:], "ha1"))
-        w2_mx.append(mx_tiles(K_PASS, "w2b"))
-        quantize(w2_mx[1], w2b, 0, P)
-        quantize(w2_mx[1], w2b, P, 2 * P)
-        quantize(w2_mx[1], w2b, 2 * P, K_PASS)
-        ha_cols = [(codes, scales, 0) for codes, scales in ha_mx]
+        first_layer(ha[1][:], xa_mx, 0, w1_mx[1], (2, 3))
+        early = [sbuf([P, 2 * P * PACK], BF16, f"w2_early{g}") for g in range(HIDDEN_PASSES)]
+        w2_low, ha_cols = [], []
+        for g in range(HIDDEN_PASSES):
+            group_planes(early[g][:], w2_raw[g], 0, 2, nc.vector.tensor_copy)
+            w2_low.append(quantized(early[g][:], f"w2_low{g}"))
+            ha_cols.append((*quantized(ha[g][:], f"ha{g}", f"w2_early{g}"), 0))
+        w2_mx = [w2_low]
         for t in range(2):
-            scatter([t], 0, QUARTER, second_layer([t], QUARTER, ha_cols, w2_mx, f"ya{t}"))
+            scatter(t, 0, QUARTER, second_layer([(t, ha_cols)], QUARTER, w2_mx, f"ya{t}", 4 + t)[:, 0, :])
         hb = [sbuf([P, QUARTER * PACK], BF16, f"hb{g}") for g in range(HIDDEN_PASSES)]
-        hb_cols = []
+        hb_codes, hb_scales = mx_tiles(HIDDEN_PASSES * QUARTER, "hb", "ha1")
+        hb_cols = [(hb_codes, hb_scales, g * QUARTER) for g in range(HIDDEN_PASSES)]
         for g in range(HIDDEN_PASSES):
-            first_layer(hb[g][:], xa_mx, QUARTER, w1_mx[g])
-            hb_cols.append((*quantized(hb[g][:], f"hb{g}"), 0))
-        scatter([2, 3], 0, QUARTER, second_layer([2, 3], QUARTER, ha_cols, w2_mx, "ya23", True))
-        scatter([0, 1], QUARTER, HALF, second_layer([0, 1], QUARTER, hb_cols, w2_mx, "yb01"))
-        hc = sbuf([P, HIDDEN_PASSES * HALF * PACK], BF16, "hc")
+            first_layer(hb[g][:], xa_mx, QUARTER, w1_mx[g], (2 * g, 2 * g + 1))
+            cols = slice(g * QUARTER, (g + 1) * QUARTER)
+            nc.vector.quantize_mx(out=hb_codes[:, cols].bitcast(FP8X4), scales=hb_scales[:, cols], in_=hb[g][:])
+        late = sbuf([P, HIDDEN_PASSES * 2 * P * PACK], BF16, "w2_late", "hb1")
         for g in range(HIDDEN_PASSES):
-            first_layer(hc[:, g * HALF * PACK : (g + 1) * HALF * PACK], xb_mx, 0, w1_mx[g])
+            group_planes(late[:, g * 2 * P * PACK : (g + 1) * 2 * P * PACK], w2_raw[g], 2, PACK, nc.scalar.copy)
+        late_mx = quantized(late[:], "w2_late")
+        w2_mx.append([(late_mx[0][:, g * 2 * P :], late_mx[1][:, g * 2 * P :]) for g in range(HIDDEN_PASSES)])
+        yb = second_layer([(0, hb_cols), (1, hb_cols)], QUARTER, w2_mx, "yb01", 6, "w2_raw1")
+        for t in range(2):
+            scatter(t, QUARTER, HALF, yb[:, t, :])
+        y2 = second_layer([(2, ha_cols), (2, hb_cols)], QUARTER, w2_mx, "ya2", 7)
+        scatter(2, 0, HALF, y2[:].rearrange("p q n -> p (q n)"))
+        hc = sbuf([P, HIDDEN_PASSES * HALF * PACK], BF16, "hc", "w2_raw0")
+        for g in range(HIDDEN_PASSES):
+            first_layer(hc[:, g * HALF * PACK : (g + 1) * HALF * PACK], xb_mx, 0, w1_mx[g], (0, 1, 4, 5))
         hc_mx = quantized(hc[:], "hc")
         hc_cols = [(hc_mx[0], hc_mx[1], g * HALF) for g in range(HIDDEN_PASSES)]
-        scatter([2, 3], QUARTER, HALF, second_layer([2, 3], QUARTER, hb_cols, w2_mx, "yb23", True))
+        y3 = second_layer([(3, ha_cols), (3, hb_cols)], QUARTER, w2_mx, "ya3", 5)
+        scatter(3, 0, HALF, y3[:].rearrange("p q n -> p (q n)"))
         for t in range(PACK):
-            scatter([t], HALF, G, second_layer([t], HALF, hc_cols, w2_mx, f"yc{t}"))
+            scatter(t, HALF, G, second_layer([(t, hc_cols)], HALF, w2_mx, f"yc{t}", (2, 3, 6, 7)[t])[:, 0, :])
             nc.sync.dma_start(out_rows[t], planes[t][:])

@@ -166,7 +166,7 @@ def tile_attend_mod_relu_kernel(tc, xT, w1, w2, offs, out):
         hb_codes, hb_scales = mx_tiles(HIDDEN_PASSES * QUARTER, "hb", "ha1")
         hb_cols = [(hb_codes, hb_scales, g * QUARTER) for g in range(HIDDEN_PASSES)]
         for g in range(HIDDEN_PASSES):
-            first_layer(hb[g][:], xa_mx, QUARTER, w1_mx[g], (2 * g, 2 * g + 1))
+            first_layer(hb[g][:], xa_mx, QUARTER, w1_mx[g], ((6, 7), (0, 1))[g])
             cols = slice(g * QUARTER, (g + 1) * QUARTER)
             nc.vector.quantize_mx(out=hb_codes[:, cols].bitcast(FP8X4), scales=hb_scales[:, cols], in_=hb[g][:])
         late = sbuf([P, HIDDEN_PASSES * 2 * P * PACK], BF16, "w2_late", "hb1")
@@ -181,11 +181,11 @@ def tile_attend_mod_relu_kernel(tc, xT, w1, w2, offs, out):
         scatter(2, 0, HALF, y2[:].rearrange("p q n -> p (q n)"))
         hc = sbuf([P, HIDDEN_PASSES * HALF * PACK], BF16, "hc", "w2_raw0")
         for g in range(HIDDEN_PASSES):
-            first_layer(hc[:, g * HALF * PACK : (g + 1) * HALF * PACK], xb_mx, 0, w1_mx[g], (0, 1, 4, 5))
+            first_layer(hc[:, g * HALF * PACK : (g + 1) * HALF * PACK], xb_mx, 0, w1_mx[g], (2, 3, 4, 5))
         hc_mx = quantized(hc[:], "hc")
         hc_cols = [(hc_mx[0], hc_mx[1], g * HALF) for g in range(HIDDEN_PASSES)]
         y3 = second_layer([(3, ha_cols), (3, hb_cols)], QUARTER, w2_mx, "ya3", 5)
         scatter(3, 0, HALF, y3[:].rearrange("p q n -> p (q n)"))
         for t in range(PACK):
-            scatter(t, HALF, G, second_layer([(t, hc_cols)], HALF, w2_mx, f"yc{t}", (2, 3, 6, 7)[t])[:, 0, :])
+            scatter(t, HALF, G, second_layer([(t, hc_cols)], HALF, w2_mx, f"yc{t}", (0, 1, 6, 7)[t])[:, 0, :])
             nc.sync.dma_start(out_rows[t], planes[t][:])

@@ -149,21 +149,21 @@ def tile_attend_mod_relu_kernel(tc, xT, w1, w2, offs, out):
         w1_mx = [quantized(w1a, "w1a")]
         xb_mx = quantized(xb[:], "xb", "w1a")
         w1b = group_weight(w1_raw[1], "w1b", 64)
-        ha = [sbuf([P, QUARTER * PACK], BF16, f"ha{g}") for g in range(HIDDEN_PASSES)]
+        both = [sbuf([P, 2 * QUARTER * PACK], BF16, f"both{g}") for g in range(HIDDEN_PASSES)]
+        ha = [tile[:, QUARTER * PACK :] for tile in both]
         first_layer(ha[0][:], xa_mx, 0, w1_mx[0], (0, 1))
         w1_mx.append(quantized(w1b, "w1b"))
         first_layer(ha[1][:], xa_mx, 0, w1_mx[1], (2, 3))
-        early = [sbuf([P, 2 * P * PACK], BF16, f"w2_early{g}") for g in range(HIDDEN_PASSES)]
         w2_low, ha_cols = [], []
         for g in range(HIDDEN_PASSES):
-            group_planes(early[g][:], w2_raw[g], 0, 2, nc.vector.tensor_copy)
-            w2_low.append(quantized(early[g][:], f"w2_low{g}"))
-            ha_cols.append((*quantized(ha[g][:], f"ha{g}", f"w2_early{g}"), 0))
+            group_planes(both[g][:, : QUARTER * PACK], w2_raw[g], 0, 2, nc.vector.tensor_copy)
+            w2_low.append(quantized(both[g][:], f"both{g}"))
+            ha_cols.append((*w2_low[g], QUARTER))
         w2_mx = [w2_low]
         for t in range(2):
             scatter(t, 0, QUARTER, second_layer([(t, ha_cols)], QUARTER, w2_mx, f"ya{t}", 4 + t)[:, 0, :])
         hb = [sbuf([P, QUARTER * PACK], BF16, f"hb{g}") for g in range(HIDDEN_PASSES)]
-        hb_codes, hb_scales = mx_tiles(HIDDEN_PASSES * QUARTER, "hb", "ha1")
+        hb_codes, hb_scales = mx_tiles(HIDDEN_PASSES * QUARTER, "hb", "both1")
         hb_cols = [(hb_codes, hb_scales, g * QUARTER) for g in range(HIDDEN_PASSES)]
         for g in range(HIDDEN_PASSES):
             first_layer(hb[g][:], xa_mx, QUARTER, w1_mx[g], ((6, 7), (0, 1))[g])

@@ -160,13 +160,15 @@ def tile_attend_mod_relu_kernel(tc, xT, w1, w2, offs, out):
             w2_low.append(quantized(both[g][:], f"both{g}"))
             ha_cols.append((*w2_low[g], QUARTER))
         w2_mx = [w2_low]
-        for t in range(2):
-            scatter(t, 0, QUARTER, second_layer([(t, ha_cols)], QUARTER, w2_mx, f"ya{t}", 4 + t)[:, 0, :])
+        for b in range(2):
+            cols = [(codes, scales, c0 + b * NB) for codes, scales, c0 in ha_cols]
+            scatter(0, b * NB, (b + 1) * NB, second_layer([(0, cols)], NB, w2_mx, f"ya0{b}", (4, 7)[b])[:, 0, :])
+        scatter(1, 0, QUARTER, second_layer([(1, ha_cols)], QUARTER, w2_mx, "ya1", 5)[:, 0, :])
         hb = [sbuf([P, QUARTER * PACK], BF16, f"hb{g}") for g in range(HIDDEN_PASSES)]
         hb_codes, hb_scales = mx_tiles(HIDDEN_PASSES * QUARTER, "hb", "both1")
         hb_cols = [(hb_codes, hb_scales, g * QUARTER) for g in range(HIDDEN_PASSES)]
         for g in range(HIDDEN_PASSES):
-            first_layer(hb[g][:], xa_mx, QUARTER, w1_mx[g], ((6, 7), (0, 1))[g])
+            first_layer(hb[g][:], xa_mx, QUARTER, w1_mx[g], ((6, 2), (0, 1))[g])
             cols = slice(g * QUARTER, (g + 1) * QUARTER)
             nc.vector.quantize_mx(out=hb_codes[:, cols].bitcast(FP8X4), scales=hb_scales[:, cols], in_=hb[g][:])
         late = sbuf([P, HIDDEN_PASSES * 2 * P * PACK], BF16, "w2_late", "hb1")
@@ -177,15 +179,15 @@ def tile_attend_mod_relu_kernel(tc, xT, w1, w2, offs, out):
         yb = second_layer([(0, hb_cols), (1, hb_cols)], QUARTER, w2_mx, "yb01", 6, "w2_raw1")
         for t in range(2):
             scatter(t, QUARTER, HALF, yb[:, t, :])
-        y2 = second_layer([(2, ha_cols), (2, hb_cols)], QUARTER, w2_mx, "ya2", 7)
+        y2 = second_layer([(2, ha_cols), (2, hb_cols)], QUARTER, w2_mx, "ya2", 2)
         scatter(2, 0, HALF, y2[:].rearrange("p q n -> p (q n)"))
         hc = sbuf([P, HIDDEN_PASSES * HALF * PACK], BF16, "hc", "w2_raw0")
         for g in range(HIDDEN_PASSES):
-            first_layer(hc[:, g * HALF * PACK : (g + 1) * HALF * PACK], xb_mx, 0, w1_mx[g], (2, 3, 4, 5))
+            first_layer(hc[:, g * HALF * PACK : (g + 1) * HALF * PACK], xb_mx, 0, w1_mx[g], (7, 5, 3, 4))
         hc_mx = quantized(hc[:], "hc")
         hc_cols = [(hc_mx[0], hc_mx[1], g * HALF) for g in range(HIDDEN_PASSES)]
-        y3 = second_layer([(3, ha_cols), (3, hb_cols)], QUARTER, w2_mx, "ya3", 5)
+        y3 = second_layer([(3, ha_cols), (3, hb_cols)], QUARTER, w2_mx, "ya3", 4)
         scatter(3, 0, HALF, y3[:].rearrange("p q n -> p (q n)"))
         for t in range(PACK):
-            scatter(t, HALF, G, second_layer([(t, hc_cols)], HALF, w2_mx, f"yc{t}", (0, 1, 6, 7)[t])[:, 0, :])
+            scatter(t, HALF, G, second_layer([(t, hc_cols)], HALF, w2_mx, f"yc{t}", (0, 1, 6, 2)[t])[:, 0, :])
             nc.sync.dma_start(out_rows[t], planes[t][:])

@@ -52,17 +52,17 @@ def tile_attend_mod_relu_kernel(tc, xT, w1, w2, offs, out):
 
         def group_weight(raw, label, split):
             grouped = sbuf([P, K_PASS * PACK], BF16, label)
-            dst = grouped[:].rearrange("p (t m j) -> p m j t", t=PACK, j=PACK)
-            src = raw[:].rearrange("p j (m t) -> p m j t", t=PACK)
+            dst = grouped[:].rearrange("p (t m i j) -> p m j i t", t=PACK, i=2, j=PACK)
+            src = raw[:].rearrange("p j (m i t) -> p m j i t", i=2, t=PACK)
             if split > 0:
-                nc.vector.tensor_copy(dst[:, :split], src[:, :split])
+                nc.vector.tensor_copy(dst[:, : split // 2], src[:, : split // 2])
             if split < P:
-                nc.scalar.copy(dst[:, split:], src[:, split:])
+                nc.scalar.copy(dst[:, split // 2 :], src[:, split // 2 :])
             return grouped[:]
 
         def group_planes(grouped, raw, t0, t1, engine):
-            dst = grouped.rearrange("p (t m j) -> p m j t", m=P, j=PACK)
-            engine(dst, raw[:].rearrange("p j (m t) -> p m j t", t=PACK)[:, :, :, t0:t1])
+            dst = grouped.rearrange("p (t m i j) -> p m j i t", m=P // 2, i=2, j=PACK)
+            engine(dst, raw[:].rearrange("p j (m i t) -> p m j i t", i=2, t=PACK)[:, :, :, :, t0:t1])
 
         def mx_tiles(width, label, tag=None):
             return sbuf([P, width], U32, f"{label}_codes", tag), sbuf([P, width], U8, f"{label}_scales")

@@ -12,6 +12,7 @@ U16 = mybir.dt.uint16
 U8 = mybir.dt.uint8
 FP8X4 = mybir.dt.float8_e4m3fn_x4
 RELU = mybir.ActivationFunctionType.Relu
+COPY = mybir.ActivationFunctionType.Copy
 ADD = mybir.AluOpType.add
 
 P = 128
@@ -21,23 +22,28 @@ HALF = 512
 QUARTER = 256
 NB = 128
 HIDDEN_PASSES = H // K_PASS
+W1_ON_VECTOR = (64, 80)
 
 
 def tile_attend_mod_relu_kernel(tc, xT, w1, w2, offs, out):
     nc = tc.nc
     with ExitStack() as ctx:
         keep = ctx.enter_context(tc.tile_pool(name="keep", bufs=1))
+        reused = ctx.enter_context(tc.tile_pool(name="reused", bufs=1))
         psum = ctx.enter_context(tc.psum_pool(name="psum", bufs=1))
 
         def sbuf(shape, dtype, label, tag=None):
+            if isinstance(tag, int):
+                return reused.tile(shape, dtype, align_bytes=64, offset=tag, name=label)
             return keep.tile(shape, dtype, align_bytes=64, tag=tag or label, name=label)
 
+        bank = [psum.tile([P, HALF], F32, name=f"bank{b}") for b in range(8)]
         offsets = keep.tile([P, G // 16], U16, name="offsets")
         x_rows = xT.rearrange("(p t) c -> t p c", t=PACK)
         out_rows = out.rearrange("(p t) c -> t p c", t=PACK)
         w1_rows = w1.rearrange("(p j) c -> p j c", j=PACK)
         planes = [sbuf([P, T], F32, f"plane{t}") for t in range(PACK)]
-        w1_raw = [sbuf([P, PACK, K_PASS], F32, f"w1_raw{g}") for g in range(HIDDEN_PASSES)]
+        w1_raw = [sbuf([P, PACK, K_PASS], F32, "w1_raw0"), sbuf([P, PACK, K_PASS], F32, "w1_raw1", 0)]
         w2_raw = [sbuf([P, PACK, D], F32, f"w2_raw{g}") for g in range(HIDDEN_PASSES)]
 
         nc.sync.dma_start(planes[0][:], x_rows[0])
@@ -50,51 +56,51 @@ def tile_attend_mod_relu_kernel(tc, xT, w1, w2, offs, out):
             rows = w2[g * K_PASS : (g + 1) * K_PASS, :].rearrange("(p j) c -> p j c", j=PACK)
             nc.sync.dma_start(w2_raw[g][:], rows)
 
-        def group_weight(raw, label, split):
-            grouped = sbuf([P, K_PASS * PACK], BF16, label)
-            dst = grouped[:].rearrange("p (t m i j) -> p m j i t", t=PACK, i=2, j=PACK)
+        def round_weight(grouped, raw, on_vector):
+            dst = grouped.rearrange("p (t m i j) -> p m j i t", t=PACK, i=2, j=PACK)
             src = raw[:].rearrange("p j (m i t) -> p m j i t", i=2, t=PACK)
-            if split > 0:
-                nc.vector.tensor_copy(dst[:, : split // 2], src[:, : split // 2])
-            if split < P:
-                nc.scalar.copy(dst[:, split // 2 :], src[:, split // 2 :])
-            return grouped[:]
-
-        def group_planes(grouped, raw, t0, t1, engine):
-            dst = grouped.rearrange("p (t m i j) -> p m j i t", m=P // 2, i=2, j=PACK)
-            engine(dst, raw[:].rearrange("p j (m i t) -> p m j i t", i=2, t=PACK)[:, :, :, :, t0:t1])
-
-        def mx_tiles(width, label, tag=None):
-            return sbuf([P, width], U32, f"{label}_codes", tag), sbuf([P, width], U8, f"{label}_scales")
-
-        def quantize(mx, grouped, c0, c1):
-            nc.vector.quantize_mx(
-                out=mx[0][:, c0:c1].bitcast(FP8X4), scales=mx[1][:, c0:c1], in_=grouped[:, c0 * PACK : c1 * PACK]
-            )
+            if on_vector < P:
+                nc.scalar.copy(dst[:, on_vector // 2 :], src[:, on_vector // 2 :])
+            nc.vector.tensor_copy(dst[:, : on_vector // 2], src[:, : on_vector // 2])
 
         def quantized(grouped, label, tag=None):
             width = grouped.shape[1] // PACK
-            mx = mx_tiles(width, label, tag)
-            quantize(mx, grouped, 0, width)
-            return mx
+            codes = sbuf([P, width], U32, f"{label}_codes", tag)
+            scales = sbuf([P, width], U8, f"{label}_scales")
+            nc.vector.quantize_mx(out=codes[:].bitcast(FP8X4), scales=scales[:], in_=grouped)
+            return codes, scales
 
-        picked = sbuf([P, PACK, G], F32, "picked")
+        picked = sbuf([P, 2, PACK, HALF], F32, "picked")
 
         def listed(t, n0, n1):
             return planes[t][:].indirect(offsets[:, n0 // 16 : n1 // 16])
 
-        def gather(t, n0, n1):
-            nc.vector.tensor_copy(picked[:, t, n0:n1], listed(t, n0, n1))
+        def vector_move(dst, src):
+            nc.vector.tensor_copy(dst, src)
 
-        def group_x(grouped, n0, n1, t0, t1):
-            dst = grouped.rearrange("p (c i t) -> p c t i", i=PACK, t=PACK)
-            nc.scalar.copy(dst[:, :, t0:t1], picked[:, t0:t1, n0:n1].rearrange("p t (c i) -> p c t i", i=PACK))
+        def scalar_move(dst, src):
+            nc.scalar.activation(dst, src, COPY)
 
-        def first_layer(grouped, x_mx, c0, w_mx, banks):
-            dst = grouped.rearrange("p (n t) -> p n t", t=PACK)
-            for b in range(dst.shape[1] // NB):
-                cols = slice(c0 + b * NB, c0 + (b + 1) * NB)
-                acc = psum.tile([P, PACK, NB], F32, tag=f"bank{banks[b]}", name="acc1")
+        def gather(move, t, n0, n1):
+            half = n0 // HALF
+            move(picked[:, half, t, n0 - half * HALF : n1 - half * HALF], listed(t, n0, n1))
+
+        def round_x(copy, grouped, half, t0, t1, n0=0, n1=HALF):
+            dst = grouped[:, n0 * PACK : n1 * PACK].rearrange("p (c i t) -> p c t i", i=PACK, t=PACK)
+            src = picked[:, half, t0:t1, n0:n1].rearrange("p t (c i) -> p c t i", i=PACK)
+            copy(dst[:, :, t0:t1], src)
+
+        def scalar_relu(dst, src):
+            nc.scalar.activation(dst, src, RELU)
+
+        def vector_relu(dst, src):
+            nc.vector.tensor_scalar_max(dst, src, 0.0)
+
+        def first_layer(hidden, x_mx, w_mx, banks, relu=scalar_relu):
+            dst = hidden.rearrange("p (n t) -> p n t", t=PACK)
+            for b in banks:
+                cols = slice(b * NB, (b + 1) * NB)
+                acc = bank[banks[b]][:].rearrange("p (t n) -> p t n", t=PACK)
                 for t in range(PACK):
                     chans = slice(t * P, (t + 1) * P)
                     nc.tensor.matmul_mx(
@@ -106,88 +112,91 @@ def tile_attend_mod_relu_kernel(tc, xT, w1, w2, offs, out):
                         start=True,
                         stop=True,
                     )
-                nc.scalar.activation(dst[:, b * NB : (b + 1) * NB, :], acc[:].rearrange("p t n -> p n t"), RELU)
+                relu(dst[:, cols, :], acc.rearrange("p t n -> p n t"))
 
-        def second_sums(parts, width, w_mx, bank):
-            acc = psum.tile([P, len(parts), width], F32, tag=f"bank{bank}", name="acc2")
-            for k, (t, h_cols) in enumerate(parts):
-                chans = slice(t % 2 * P, (t % 2 + 1) * P)
+        totals = {}
+
+        def second_layer(first, second, b):
+            acc = bank[b][:].rearrange("p (k n) -> p k n", k=2)
+            for k, (t, q) in enumerate((first, second)):
+                cols = slice(q % 2 * QUARTER, (q % 2 + 1) * QUARTER)
                 for g in range(HIDDEN_PASSES):
-                    codes, scales, c0 = h_cols[g]
+                    chans = slice(g * D + t * P, g * D + (t + 1) * P)
+                    codes, scales = h_mx[q // 2][g]
                     nc.tensor.matmul_mx(
                         out=acc[:, k, :],
-                        lhsT=w_mx[t // 2][g][0][:, chans].bitcast(FP8X4),
-                        lhsT_scale=w_mx[t // 2][g][1][:, chans],
-                        rhs=codes[:, c0 : c0 + width].bitcast(FP8X4),
-                        rhs_scale=scales[:, c0 : c0 + width],
+                        lhsT=w2_mx[0][:, chans].bitcast(FP8X4),
+                        lhsT_scale=w2_mx[1][:, chans],
+                        rhs=codes[:, cols].bitcast(FP8X4),
+                        rhs_scale=scales[:, cols],
                         start=(g == 0),
                         stop=(g == HIDDEN_PASSES - 1),
                     )
-            return acc
+            at = [(q // 2 * PACK + t) * 2 + q % 2 for t, q in (first, second)]
+            quarters = picked[:].rearrange("p h t (i n) -> p (h t i) n", i=2)
+            residual = quarters[:, at[0] : at[1] + 1 : at[1] - at[0], :]
+            total = sbuf([P, 2, QUARTER], F32, f"total{first[0]}{first[1]}")
+            nc.vector.tensor_tensor(total[:], acc, residual, ADD)
+            totals[first], totals[second] = total[:, 0, :], total[:, 1, :]
+            return total[:].rearrange("p k n -> p (k n)")
 
-        def second_layer(parts, width, w_mx, label, bank, tag=None):
-            acc = second_sums(parts, width, w_mx, bank)
-            product = sbuf([P, len(parts), width], F32, label, tag)
-            nc.scalar.copy(product[:], acc[:])
-            return product
+        def scalar_scatter(t, q):
+            scalar_move(listed(t, q * QUARTER, (q + 1) * QUARTER), totals[t, q])
 
-        def scatter(t, n0, n1, product):
-            nc.vector.tensor_tensor(listed(t, n0, n1), product, picked[:, t, n0:n1], ADD)
-
-        for t in range(PACK - 1):
-            gather(t, 0, G)
-        gather(PACK - 1, 0, HALF)
-        gather(PACK - 1, HALF, G)
         xa = sbuf([P, HALF * PACK], BF16, "xa")
         xb = sbuf([P, HALF * PACK], BF16, "xb")
-        group_x(xa[:], 0, HALF, 0, 2)
-        group_x(xb[:], HALF, G, 0, 2)
-        group_x(xa[:], 0, HALF, 2, 4)
-        group_x(xb[:], HALF, G, 2, 4)
-        w1a = group_weight(w1_raw[0], "w1a", P)
-        xa_mx = quantized(xa[:], "xa", "w1_raw0")
-        w1_mx = [quantized(w1a, "w1a")]
-        xb_mx = quantized(xb[:], "xb", "w1a")
-        w1b = group_weight(w1_raw[1], "w1b", 64)
-        both = [sbuf([P, 2 * QUARTER * PACK], BF16, f"both{g}") for g in range(HIDDEN_PASSES)]
-        ha = [tile[:, QUARTER * PACK :] for tile in both]
-        first_layer(ha[0][:], xa_mx, 0, w1_mx[0], (0, 1))
-        w1_mx.append(quantized(w1b, "w1b"))
-        first_layer(ha[1][:], xa_mx, 0, w1_mx[1], (2, 3))
-        w2_low, ha_cols = [], []
+        gather(vector_move, 0, 0, HALF)
+        round_x(nc.scalar.copy, xa[:], 0, 0, 1, 0, QUARTER)
+        gather(vector_move, 0, HALF, G)
+        gather(vector_move, 1, 0, HALF)
+        gather(scalar_move, 1, HALF, G)
+        round_x(nc.scalar.copy, xa[:], 0, 1, 2, 0, QUARTER)
+        round_x(nc.vector.tensor_copy, xa[:], 0, 0, 2, QUARTER, HALF)
+        round_x(nc.vector.tensor_copy, xb[:], 1, 0, 2)
+        gather(vector_move, 2, 0, HALF)
+        gather(scalar_move, 2, HALF, G)
+        gather(vector_move, 3, 0, QUARTER)
+        gather(scalar_move, 3, QUARTER, HALF)
+        gather(scalar_move, 3, HALF, G)
+        round_x(nc.vector.tensor_copy, xa[:], 0, 2, 4)
+        round_x(nc.scalar.copy, xb[:], 1, 2, 4, 0, QUARTER)
+        round_x(nc.vector.tensor_copy, xb[:], 1, 2, 4, QUARTER, HALF)
+        xa_mx = quantized(xa[:], "xa")
+        w1a = sbuf([P, K_PASS * PACK], BF16, "w1a")
+        round_weight(w1a[:], w1_raw[0], W1_ON_VECTOR[0])
+        w1a_mx = quantized(w1a[:], "w1a")
+        w1b = sbuf([P, K_PASS * PACK], BF16, "w1b")
+        round_weight(w1b[:], w1_raw[1], W1_ON_VECTOR[1])
+        ha = [sbuf([P, HALF * PACK], BF16, "ha0", 0)[:], sbuf([P, HALF * PACK], BF16, "ha1")[:]]
+        hb = [sbuf([P, HALF * PACK], BF16, f"hb{g}")[:] for g in range(HIDDEN_PASSES)]
+        rotation = {b: b for b in range(HALF // NB)}
+        first_layer(ha[0], xa_mx, w1a_mx, rotation)
+        xb_mx = quantized(xb[:], "xb", HALF * PACK * 2)
+        w1b_mx = quantized(w1b[:], "w1b")
+        first_layer(ha[1], xa_mx, w1b_mx, rotation)
+        first_layer(hb[0], xb_mx, w1a_mx, rotation)
+        first_layer(hb[1], xb_mx, w1b_mx, {0: 0, 1: 1, 2: 2})
+        w2g = sbuf([P, HIDDEN_PASSES * D * PACK], BF16, "w2g")
+        h_mx = [[], []]
         for g in range(HIDDEN_PASSES):
-            group_planes(both[g][:, : QUARTER * PACK], w2_raw[g], 0, 2, nc.vector.tensor_copy)
-            w2_low.append(quantized(both[g][:], f"both{g}"))
-            ha_cols.append((*w2_low[g], QUARTER))
-        w2_mx = [w2_low]
-        for b in range(2):
-            cols = [(codes, scales, c0 + b * NB) for codes, scales, c0 in ha_cols]
-            scatter(0, b * NB, (b + 1) * NB, second_layer([(0, cols)], NB, w2_mx, f"ya0{b}", (4, 7)[b])[:, 0, :])
-        scatter(1, 0, QUARTER, second_layer([(1, ha_cols)], QUARTER, w2_mx, "ya1", 5)[:, 0, :])
-        hb = [sbuf([P, QUARTER * PACK], BF16, f"hb{g}") for g in range(HIDDEN_PASSES)]
-        hb_codes, hb_scales = mx_tiles(HIDDEN_PASSES * QUARTER, "hb", "both1")
-        hb_cols = [(hb_codes, hb_scales, g * QUARTER) for g in range(HIDDEN_PASSES)]
-        for g in range(HIDDEN_PASSES):
-            first_layer(hb[g][:], xa_mx, QUARTER, w1_mx[g], ((6, 2), (0, 1))[g])
-            cols = slice(g * QUARTER, (g + 1) * QUARTER)
-            nc.vector.quantize_mx(out=hb_codes[:, cols].bitcast(FP8X4), scales=hb_scales[:, cols], in_=hb[g][:])
-        late = sbuf([P, HIDDEN_PASSES * 2 * P * PACK], BF16, "w2_late", "hb1")
-        for g in range(HIDDEN_PASSES):
-            group_planes(late[:, g * 2 * P * PACK : (g + 1) * 2 * P * PACK], w2_raw[g], 2, PACK, nc.scalar.copy)
-        late_mx = quantized(late[:], "w2_late")
-        w2_mx.append([(late_mx[0][:, g * 2 * P :], late_mx[1][:, g * 2 * P :]) for g in range(HIDDEN_PASSES)])
-        yb = second_layer([(0, hb_cols), (1, hb_cols)], QUARTER, w2_mx, "yb01", 6, "w2_raw1")
-        for t in range(2):
-            scatter(t, QUARTER, HALF, yb[:, t, :])
-        y2 = second_layer([(2, ha_cols), (2, hb_cols)], QUARTER, w2_mx, "ya2", 2)
-        scatter(2, 0, HALF, y2[:].rearrange("p q n -> p (q n)"))
-        hc = sbuf([P, HIDDEN_PASSES * HALF * PACK], BF16, "hc", "w2_raw0")
-        for g in range(HIDDEN_PASSES):
-            first_layer(hc[:, g * HALF * PACK : (g + 1) * HALF * PACK], xb_mx, 0, w1_mx[g], (7, 5, 3, 4))
-        hc_mx = quantized(hc[:], "hc")
-        hc_cols = [(hc_mx[0], hc_mx[1], g * HALF) for g in range(HIDDEN_PASSES)]
-        y3 = second_layer([(3, ha_cols), (3, hb_cols)], QUARTER, w2_mx, "ya3", 4)
-        scatter(3, 0, HALF, y3[:].rearrange("p q n -> p (q n)"))
-        for t in range(PACK):
-            scatter(t, HALF, G, second_layer([(t, hc_cols)], HALF, w2_mx, f"yc{t}", (0, 1, 6, 2)[t])[:, 0, :])
+            round_weight(w2g[:, g * D * PACK : (g + 1) * D * PACK], w2_raw[g], P)
+            h_mx[0].append(quantized(ha[g], f"ha{g}", f"w2_raw{g}"))
+        w2_mx = quantized(w2g[:], "w2")
+        h_mx[1].append(quantized(hb[0], "hb0", "w2g"))
+        second_layer((1, 0), (2, 0), 4)
+        first_half = second_layer((0, 0), (0, 1), 7)
+        first_layer(hb[1], xb_mx, w1b_mx, {3: 4}, vector_relu)
+        second_layer((1, 1), (2, 1), 5)
+        h_mx[1].append(quantized(hb[1], "hb1"))
+        vector_move(listed(0, 0, HALF), first_half)
+        second_layer((3, 0), (2, 2), 6)
+        second_half = second_layer((0, 2), (0, 3), 3)
+        second_layer((3, 1), (2, 3), 4)
+        vector_move(listed(0, HALF, G), second_half)
+        last_half = second_layer((1, 2), (1, 3), 5)
+        second_layer((3, 2), (3, 3), 6)
+        for t, q in ((2, 0), (1, 0), (2, 1), (1, 1), (2, 2), (3, 0), (2, 3), (3, 1), (3, 2), (3, 3)):
+            scalar_scatter(t, q)
+        vector_move(listed(1, HALF, G), last_half)
+        for t in (0, 2, 1, 3):
             nc.sync.dma_start(out_rows[t], planes[t][:])

@@ -22,7 +22,10 @@ HALF = 512
 QUARTER = 256
 NB = 128
 HIDDEN_PASSES = H // K_PASS
-W1_ON_VECTOR = (64, 80)
+RAW_BYTES = PACK * K_PASS * 4
+W1_ON_VECTOR = 88
+PLANE0_ON_SCALAR = 288
+SCALAR_PIECES = ((0, 256), (256, 640), (640, 1024))
 
 
 def tile_attend_mod_relu_kernel(tc, xT, w1, w2, offs, out):
@@ -43,25 +46,26 @@ def tile_attend_mod_relu_kernel(tc, xT, w1, w2, offs, out):
         out_rows = out.rearrange("(p t) c -> t p c", t=PACK)
         w1_rows = w1.rearrange("(p j) c -> p j c", j=PACK)
         planes = [sbuf([P, T], F32, f"plane{t}") for t in range(PACK)]
-        w1_raw = [sbuf([P, PACK, K_PASS], F32, "w1_raw0"), sbuf([P, PACK, K_PASS], F32, "w1_raw1", 0)]
-        w2_raw = [sbuf([P, PACK, D], F32, f"w2_raw{g}") for g in range(HIDDEN_PASSES)]
+        w1a_raw = sbuf([P, PACK, K_PASS], F32, "w1a_raw", 0)
+        w1b_raw = [sbuf([P, PACK, K_PASS // 2], F32, f"w1b_raw{u}") for u in range(2)]
+        w2_raw = [sbuf([P, PACK, D], F32, "w2_raw0"), sbuf([P, PACK, D], F32, "w2_raw1", RAW_BYTES)]
 
         nc.sync.dma_start(planes[0][:], x_rows[0])
         nc.sync.dma_start(offsets[:], offs)
         for t in range(1, PACK):
             nc.sync.dma_start(planes[t][:], x_rows[t])
-        for g in range(HIDDEN_PASSES):
-            nc.sync.dma_start(w1_raw[g][:], w1_rows[:, :, g * K_PASS : (g + 1) * K_PASS])
+        nc.sync.dma_start(w1a_raw[:], w1_rows[:, :, :K_PASS])
+        for u in range(2):
+            c0 = K_PASS + u * K_PASS // 2
+            nc.sync.dma_start(w1b_raw[u][:], w1_rows[:, :, c0 : c0 + K_PASS // 2])
         for g in range(HIDDEN_PASSES):
             rows = w2[g * K_PASS : (g + 1) * K_PASS, :].rearrange("(p j) c -> p j c", j=PACK)
             nc.sync.dma_start(w2_raw[g][:], rows)
 
-        def round_weight(grouped, raw, on_vector):
+        def round_weight(copy, grouped, m0, m1, raw, raw_m0=0):
             dst = grouped.rearrange("p (t m i j) -> p m j i t", t=PACK, i=2, j=PACK)
             src = raw[:].rearrange("p j (m i t) -> p m j i t", i=2, t=PACK)
-            if on_vector < P:
-                nc.scalar.copy(dst[:, on_vector // 2 :], src[:, on_vector // 2 :])
-            nc.vector.tensor_copy(dst[:, : on_vector // 2], src[:, : on_vector // 2])
+            copy(dst[:, m0 // 2 : m1 // 2], src[:, (m0 - raw_m0) // 2 : (m1 - raw_m0) // 2])
 
         def quantized(grouped, label, tag=None):
             width = grouped.shape[1] // PACK
@@ -69,6 +73,9 @@ def tile_attend_mod_relu_kernel(tc, xT, w1, w2, offs, out):
             scales = sbuf([P, width], U8, f"{label}_scales")
             nc.vector.quantize_mx(out=codes[:].bitcast(FP8X4), scales=scales[:], in_=grouped)
             return codes, scales
+
+        def by_pass(mx):
+            return [(mx[0][:, g * HALF : (g + 1) * HALF], mx[1][:, g * HALF : (g + 1) * HALF]) for g in range(HIDDEN_PASSES)]
 
         picked = sbuf([P, 2, PACK, HALF], F32, "picked")
 
@@ -114,34 +121,35 @@ def tile_attend_mod_relu_kernel(tc, xT, w1, w2, offs, out):
                     )
                 relu(dst[:, cols, :], acc.rearrange("p t n -> p n t"))
 
-        totals = {}
+        def product(acc, t, half, cols):
+            for g in range(HIDDEN_PASSES):
+                chans = slice(t * P, (t + 1) * P)
+                codes, scales = h_mx[half][g]
+                nc.tensor.matmul_mx(
+                    out=acc,
+                    lhsT=w2_mx[g][0][:, chans].bitcast(FP8X4),
+                    lhsT_scale=w2_mx[g][1][:, chans],
+                    rhs=codes[:, cols].bitcast(FP8X4),
+                    rhs_scale=scales[:, cols],
+                    start=(g == 0),
+                    stop=(g == HIDDEN_PASSES - 1),
+                )
 
-        def second_layer(first, second, b):
+        totals = sbuf([P, PACK, G], F32, "totals")
+
+        def half_sum(t, half, b):
+            product(bank[b][:], t, half, slice(0, HALF))
+            nc.vector.tensor_tensor(totals[:, t, half * HALF : (half + 1) * HALF], bank[b][:], picked[:, half, t, :], ADD)
+
+        def pair_sum(q, b):
             acc = bank[b][:].rearrange("p (k n) -> p k n", k=2)
-            for k, (t, q) in enumerate((first, second)):
-                cols = slice(q % 2 * QUARTER, (q % 2 + 1) * QUARTER)
-                for g in range(HIDDEN_PASSES):
-                    chans = slice(g * D + t * P, g * D + (t + 1) * P)
-                    codes, scales = h_mx[q // 2][g]
-                    nc.tensor.matmul_mx(
-                        out=acc[:, k, :],
-                        lhsT=w2_mx[0][:, chans].bitcast(FP8X4),
-                        lhsT_scale=w2_mx[1][:, chans],
-                        rhs=codes[:, cols].bitcast(FP8X4),
-                        rhs_scale=scales[:, cols],
-                        start=(g == 0),
-                        stop=(g == HIDDEN_PASSES - 1),
-                    )
-            at = [(q // 2 * PACK + t) * 2 + q % 2 for t, q in (first, second)]
-            quarters = picked[:].rearrange("p h t (i n) -> p (h t i) n", i=2)
-            residual = quarters[:, at[0] : at[1] + 1 : at[1] - at[0], :]
-            total = sbuf([P, 2, QUARTER], F32, f"total{first[0]}{first[1]}")
-            nc.vector.tensor_tensor(total[:], acc, residual, ADD)
-            totals[first], totals[second] = total[:, 0, :], total[:, 1, :]
-            return total[:].rearrange("p k n -> p (k n)")
+            cols = slice(q % 2 * QUARTER, (q % 2 + 1) * QUARTER)
+            for k in range(2):
+                product(acc[:, k, :], 1 + k, q // 2, cols)
+            nc.vector.tensor_tensor(totals[:, 1:3, q * QUARTER : (q + 1) * QUARTER], acc, picked[:, q // 2, 1:3, cols], ADD)
 
-        def scalar_scatter(t, q):
-            scalar_move(listed(t, q * QUARTER, (q + 1) * QUARTER), totals[t, q])
+        def scatter(move, t, n0, n1):
+            move(listed(t, n0, n1), totals[:, t, n0:n1])
 
         xa = sbuf([P, HALF * PACK], BF16, "xa")
         xb = sbuf([P, HALF * PACK], BF16, "xb")
@@ -157,46 +165,50 @@ def tile_attend_mod_relu_kernel(tc, xT, w1, w2, offs, out):
         gather(scalar_move, 2, HALF, G)
         gather(vector_move, 3, 0, QUARTER)
         gather(scalar_move, 3, QUARTER, HALF)
-        gather(scalar_move, 3, HALF, G)
+        gather(scalar_move, 3, HALF, HALF + QUARTER)
+        gather(scalar_move, 3, HALF + QUARTER, G)
         round_x(nc.vector.tensor_copy, xa[:], 0, 2, 4)
-        round_x(nc.scalar.copy, xb[:], 1, 2, 4, 0, QUARTER)
-        round_x(nc.vector.tensor_copy, xb[:], 1, 2, 4, QUARTER, HALF)
+        round_x(nc.vector.tensor_copy, xb[:], 1, 2, 4, 0, QUARTER)
+        round_x(nc.scalar.copy, xb[:], 1, 2, 4, QUARTER, HALF)
         xa_mx = quantized(xa[:], "xa")
         w1a = sbuf([P, K_PASS * PACK], BF16, "w1a")
-        round_weight(w1a[:], w1_raw[0], W1_ON_VECTOR[0])
+        round_weight(nc.scalar.copy, w1a[:], W1_ON_VECTOR, P, w1a_raw)
+        round_weight(nc.vector.tensor_copy, w1a[:], 0, W1_ON_VECTOR, w1a_raw)
         w1a_mx = quantized(w1a[:], "w1a")
+        xb_mx = quantized(xb[:], "xb", 0)
         w1b = sbuf([P, K_PASS * PACK], BF16, "w1b")
-        round_weight(w1b[:], w1_raw[1], W1_ON_VECTOR[1])
-        ha = [sbuf([P, HALF * PACK], BF16, "ha0", 0)[:], sbuf([P, HALF * PACK], BF16, "ha1")[:]]
+        round_weight(nc.scalar.copy, w1b[:], 0, P // 2, w1b_raw[0])
+        round_weight(nc.vector.tensor_copy, w1b[:], P // 2, P, w1b_raw[1], P // 2)
+        ha = sbuf([P, HIDDEN_PASSES * HALF * PACK], BF16, "ha", "w1b_raw0")
         hb = [sbuf([P, HALF * PACK], BF16, f"hb{g}")[:] for g in range(HIDDEN_PASSES)]
-        rotation = {b: b for b in range(HALF // NB)}
-        first_layer(ha[0], xa_mx, w1a_mx, rotation)
-        xb_mx = quantized(xb[:], "xb", HALF * PACK * 2)
+        first_layer(ha[:, : HALF * PACK], xa_mx, w1a_mx, {0: 4}, vector_relu)
+        first_layer(ha[:, : HALF * PACK], xa_mx, w1a_mx, {1: 0, 2: 1, 3: 2})
+        first_layer(hb[0], xb_mx, w1a_mx, {0: 3})
         w1b_mx = quantized(w1b[:], "w1b")
-        first_layer(ha[1], xa_mx, w1b_mx, rotation)
-        first_layer(hb[0], xb_mx, w1a_mx, rotation)
-        first_layer(hb[1], xb_mx, w1b_mx, {0: 0, 1: 1, 2: 2})
+        first_layer(ha[:, HALF * PACK :], xa_mx, w1b_mx, {0: 0, 1: 1, 2: 2, 3: 3})
+        first_layer(hb[0], xb_mx, w1a_mx, {1: 0, 2: 1, 3: 2})
+        first_layer(hb[1], xb_mx, w1b_mx, {0: 3, 1: 0, 2: 1})
         w2g = sbuf([P, HIDDEN_PASSES * D * PACK], BF16, "w2g")
-        h_mx = [[], []]
         for g in range(HIDDEN_PASSES):
-            round_weight(w2g[:, g * D * PACK : (g + 1) * D * PACK], w2_raw[g], P)
-            h_mx[0].append(quantized(ha[g], f"ha{g}", f"w2_raw{g}"))
-        w2_mx = quantized(w2g[:], "w2")
-        h_mx[1].append(quantized(hb[0], "hb0", "w2g"))
-        second_layer((1, 0), (2, 0), 4)
-        first_half = second_layer((0, 0), (0, 1), 7)
-        first_layer(hb[1], xb_mx, w1b_mx, {3: 4}, vector_relu)
-        second_layer((1, 1), (2, 1), 5)
+            round_weight(nc.vector.tensor_copy, w2g[:, g * D * PACK : (g + 1) * D * PACK], 0, P, w2_raw[g])
+        w2_mx = by_pass(quantized(w2g[:], "w2"))
+        h_mx = [by_pass(quantized(ha[:], "ha", RAW_BYTES))]
+        h_mx.append([quantized(hb[0], "hb0", RAW_BYTES + HIDDEN_PASSES * HALF * 4)])
+        half_sum(0, 0, 2)
+        pair_sum(0, 6)
+        first_layer(hb[1], xb_mx, w1b_mx, {3: 2}, vector_relu)
+        half_sum(3, 0, 4)
         h_mx[1].append(quantized(hb[1], "hb1"))
-        vector_move(listed(0, 0, HALF), first_half)
-        second_layer((3, 0), (2, 2), 6)
-        second_half = second_layer((0, 2), (0, 3), 3)
-        second_layer((3, 1), (2, 3), 4)
-        vector_move(listed(0, HALF, G), second_half)
-        last_half = second_layer((1, 2), (1, 3), 5)
-        second_layer((3, 2), (3, 3), 6)
-        for t, q in ((2, 0), (1, 0), (2, 1), (1, 1), (2, 2), (3, 0), (2, 3), (3, 1), (3, 2), (3, 3)):
-            scalar_scatter(t, q)
-        vector_move(listed(1, HALF, G), last_half)
-        for t in (0, 2, 1, 3):
-            nc.sync.dma_start(out_rows[t], planes[t][:])
+        pair_sum(1, 2)
+        pair_sum(2, 5)
+        pair_sum(3, 6)
+        half_sum(0, 1, 7)
+        half_sum(3, 1, 5)
+        scatter(scalar_move, 0, 0, PLANE0_ON_SCALAR)
+        for n0, n1 in SCALAR_PIECES:
+            for t in (1, 2):
+                scatter(scalar_move, t, n0, n1)
+        scatter(vector_move, 0, PLANE0_ON_SCALAR, G)
+        scatter(vector_move, 3, 0, G)
+        for t, queue in enumerate((nc.sync, nc.scalar, nc.scalar, nc.sync)):
+            queue.dma_start(out_rows[t], planes[t][:])

@@ -24,6 +24,7 @@ NB = 128
 HIDDEN_PASSES = H // K_PASS
 RAW_BYTES = PACK * K_PASS * 4
 W1_ON_VECTOR = 88
+W1B_ON_VECTOR = 76
 PLANE0_ON_SCALAR = 288
 SCALAR_PIECES = ((0, 256), (256, 640), (640, 1024))
 
@@ -46,18 +47,16 @@ def tile_attend_mod_relu_kernel(tc, xT, w1, w2, offs, out):
         out_rows = out.rearrange("(p t) c -> t p c", t=PACK)
         w1_rows = w1.rearrange("(p j) c -> p j c", j=PACK)
         planes = [sbuf([P, T], F32, f"plane{t}") for t in range(PACK)]
-        w1a_raw = sbuf([P, PACK, K_PASS], F32, "w1a_raw", 0)
-        w1b_raw = [sbuf([P, PACK, K_PASS // 2], F32, f"w1b_raw{u}") for u in range(2)]
-        w2_raw = [sbuf([P, PACK, D], F32, "w2_raw0"), sbuf([P, PACK, D], F32, "w2_raw1", RAW_BYTES)]
+        w1a_raw = sbuf([P, PACK, K_PASS], F32, "w1a_raw")
+        w1b_raw = sbuf([P, PACK, K_PASS], F32, "w1b_raw", 0)
+        w2_raw = [sbuf([P, PACK, D], F32, "w2_raw0"), sbuf([P, PACK, D], F32, "w2_raw1", 2 * RAW_BYTES)]
 
         nc.sync.dma_start(planes[0][:], x_rows[0])
         nc.sync.dma_start(offsets[:], offs)
         for t in range(1, PACK):
             nc.sync.dma_start(planes[t][:], x_rows[t])
         nc.sync.dma_start(w1a_raw[:], w1_rows[:, :, :K_PASS])
-        for u in range(2):
-            c0 = K_PASS + u * K_PASS // 2
-            nc.sync.dma_start(w1b_raw[u][:], w1_rows[:, :, c0 : c0 + K_PASS // 2])
+        nc.sync.dma_start(w1b_raw[:], w1_rows[:, :, K_PASS:])
         for g in range(HIDDEN_PASSES):
             rows = w2[g * K_PASS : (g + 1) * K_PASS, :].rearrange("(p j) c -> p j c", j=PACK)
             nc.sync.dma_start(w2_raw[g][:], rows)
@@ -175,25 +174,24 @@ def tile_attend_mod_relu_kernel(tc, xT, w1, w2, offs, out):
         round_weight(nc.scalar.copy, w1a[:], W1_ON_VECTOR, P, w1a_raw)
         round_weight(nc.vector.tensor_copy, w1a[:], 0, W1_ON_VECTOR, w1a_raw)
         w1a_mx = quantized(w1a[:], "w1a")
-        xb_mx = quantized(xb[:], "xb", 0)
         w1b = sbuf([P, K_PASS * PACK], BF16, "w1b")
-        round_weight(nc.scalar.copy, w1b[:], 0, P // 2, w1b_raw[0])
-        round_weight(nc.vector.tensor_copy, w1b[:], P // 2, P, w1b_raw[1], P // 2)
-        ha = sbuf([P, HIDDEN_PASSES * HALF * PACK], BF16, "ha", "w1b_raw0")
+        round_weight(nc.scalar.copy, w1b[:], W1B_ON_VECTOR, P, w1b_raw)
+        round_weight(nc.vector.tensor_copy, w1b[:], 0, W1B_ON_VECTOR, w1b_raw)
+        ha = sbuf([P, HIDDEN_PASSES * HALF * PACK], BF16, "ha", RAW_BYTES // 2)
         hb = [sbuf([P, HALF * PACK], BF16, f"hb{g}")[:] for g in range(HIDDEN_PASSES)]
         first_layer(ha[:, : HALF * PACK], xa_mx, w1a_mx, {0: 4}, vector_relu)
         first_layer(ha[:, : HALF * PACK], xa_mx, w1a_mx, {1: 0, 2: 1, 3: 2})
-        first_layer(hb[0], xb_mx, w1a_mx, {0: 3})
         w1b_mx = quantized(w1b[:], "w1b")
-        first_layer(ha[:, HALF * PACK :], xa_mx, w1b_mx, {0: 0, 1: 1, 2: 2, 3: 3})
-        first_layer(hb[0], xb_mx, w1a_mx, {1: 0, 2: 1, 3: 2})
+        xb_mx = quantized(xb[:], "xb", 0)
+        first_layer(ha[:, HALF * PACK :], xa_mx, w1b_mx, {0: 3, 1: 0, 2: 1, 3: 2})
+        first_layer(hb[0], xb_mx, w1a_mx, {0: 3, 1: 0, 2: 1, 3: 2})
         first_layer(hb[1], xb_mx, w1b_mx, {0: 3, 1: 0, 2: 1})
         w2g = sbuf([P, HIDDEN_PASSES * D * PACK], BF16, "w2g")
         for g in range(HIDDEN_PASSES):
             round_weight(nc.vector.tensor_copy, w2g[:, g * D * PACK : (g + 1) * D * PACK], 0, P, w2_raw[g])
         w2_mx = by_pass(quantized(w2g[:], "w2"))
-        h_mx = [by_pass(quantized(ha[:], "ha", RAW_BYTES))]
-        h_mx.append([quantized(hb[0], "hb0", RAW_BYTES + HIDDEN_PASSES * HALF * 4)])
+        h_mx = [by_pass(quantized(ha[:], "ha", 2 * RAW_BYTES))]
+        h_mx.append([quantized(hb[0], "hb0", 2 * RAW_BYTES + HIDDEN_PASSES * HALF * 4)])
         half_sum(0, 0, 2)
         pair_sum(0, 6)
         first_layer(hb[1], xb_mx, w1b_mx, {3: 2}, vector_relu)

@@ -25,7 +25,7 @@ HIDDEN_PASSES = H // K_PASS
 RAW_BYTES = PACK * K_PASS * 4
 W1_ON_VECTOR = 88
 W1B_ON_VECTOR = 76
-PLANE0_ON_SCALAR = 288
+PLANE0_ON_SCALAR = 320
 SCALAR_PIECES = ((0, 256), (256, 640), (640, 1024))
 
 
@@ -177,29 +177,31 @@ def tile_attend_mod_relu_kernel(tc, xT, w1, w2, offs, out):
         w1b = sbuf([P, K_PASS * PACK], BF16, "w1b")
         round_weight(nc.scalar.copy, w1b[:], W1B_ON_VECTOR, P, w1b_raw)
         round_weight(nc.vector.tensor_copy, w1b[:], 0, W1B_ON_VECTOR, w1b_raw)
-        ha = sbuf([P, HIDDEN_PASSES * HALF * PACK], BF16, "ha", RAW_BYTES // 2)
+        joint = [sbuf([P, 2, HALF * PACK], BF16, "joint0", RAW_BYTES // 2), sbuf([P, 2, HALF * PACK], BF16, "joint1")]
         hb = [sbuf([P, HALF * PACK], BF16, f"hb{g}")[:] for g in range(HIDDEN_PASSES)]
-        first_layer(ha[:, : HALF * PACK], xa_mx, w1a_mx, {0: 4}, vector_relu)
-        first_layer(ha[:, : HALF * PACK], xa_mx, w1a_mx, {1: 0, 2: 1, 3: 2})
+        rotation = {b: b for b in range(HALF // NB)}
+        first_layer(joint[0][:, 0, :], xa_mx, w1a_mx, rotation)
         w1b_mx = quantized(w1b[:], "w1b")
         xb_mx = quantized(xb[:], "xb", 0)
-        first_layer(ha[:, HALF * PACK :], xa_mx, w1b_mx, {0: 3, 1: 0, 2: 1, 3: 2})
-        first_layer(hb[0], xb_mx, w1a_mx, {0: 3, 1: 0, 2: 1, 3: 2})
-        first_layer(hb[1], xb_mx, w1b_mx, {0: 3, 1: 0, 2: 1})
-        w2g = sbuf([P, HIDDEN_PASSES * D * PACK], BF16, "w2g")
+        first_layer(joint[1][:, 0, :], xa_mx, w1b_mx, rotation)
+        first_layer(hb[0], xb_mx, w1a_mx, rotation)
+        first_layer(hb[1], xb_mx, w1b_mx, {0: 0, 1: 1})
+        w2_mx = []
+        h_mx = [[]]
         for g in range(HIDDEN_PASSES):
-            round_weight(nc.vector.tensor_copy, w2g[:, g * D * PACK : (g + 1) * D * PACK], 0, P, w2_raw[g])
-        w2_mx = by_pass(quantized(w2g[:], "w2"))
-        h_mx = [by_pass(quantized(ha[:], "ha", 2 * RAW_BYTES))]
+            round_weight(nc.vector.tensor_copy, joint[g][:, 1, :], 0, P, w2_raw[g])
+            h_part, w2_part = by_pass(quantized(joint[g][:].rearrange("p k n -> p (k n)"), f"joint{g}"))
+            h_mx[0].append(h_part)
+            w2_mx.append(w2_part)
         h_mx.append([quantized(hb[0], "hb0", 2 * RAW_BYTES + HIDDEN_PASSES * HALF * 4)])
         half_sum(0, 0, 2)
         pair_sum(0, 6)
-        first_layer(hb[1], xb_mx, w1b_mx, {3: 2}, vector_relu)
+        first_layer(hb[1], xb_mx, w1b_mx, {2: 2, 3: 6}, vector_relu)
         half_sum(3, 0, 4)
         h_mx[1].append(quantized(hb[1], "hb1"))
         pair_sum(1, 2)
         pair_sum(2, 5)
-        pair_sum(3, 6)
+        pair_sum(3, 3)
         half_sum(0, 1, 7)
         half_sum(3, 1, 5)
         scatter(scalar_move, 0, 0, PLANE0_ON_SCALAR)

@@ -25,7 +25,7 @@ HIDDEN_PASSES = H // K_PASS
 RAW_BYTES = PACK * K_PASS * 4
 W1_ON_VECTOR = 88
 W1B_ON_VECTOR = 76
-PLANE0_ON_SCALAR = 320
+PLANE0_ON_SCALAR = 352
 SCALAR_PIECES = ((0, 256), (256, 640), (640, 1024))
 
 
@@ -186,13 +186,12 @@ def tile_attend_mod_relu_kernel(tc, xT, w1, w2, offs, out):
         first_layer(joint[1][:, 0, :], xa_mx, w1b_mx, rotation)
         first_layer(hb[0], xb_mx, w1a_mx, rotation)
         first_layer(hb[1], xb_mx, w1b_mx, {0: 0, 1: 1})
-        w2_mx = []
-        h_mx = [[]]
-        for g in range(HIDDEN_PASSES):
-            round_weight(nc.vector.tensor_copy, joint[g][:, 1, :], 0, P, w2_raw[g])
-            h_part, w2_part = by_pass(quantized(joint[g][:].rearrange("p k n -> p (k n)"), f"joint{g}"))
-            h_mx[0].append(h_part)
-            w2_mx.append(w2_part)
+        round_weight(nc.vector.tensor_copy, joint[0][:, 1, :], 0, P, w2_raw[0])
+        h_mx = [[quantized(joint[0][:, 0, :], "ha0")]]
+        w2_mx = [quantized(joint[0][:, 1, :], "w2a")]
+        round_weight(nc.vector.tensor_copy, joint[1][:, 1, :], 0, P, w2_raw[1])
+        h_mx[0].append(quantized(joint[1][:, 0, :], "ha1"))
+        w2_mx.append(quantized(joint[1][:, 1, :], "w2b"))
         h_mx.append([quantized(hb[0], "hb0", 2 * RAW_BYTES + HIDDEN_PASSES * HALF * 4)])
         half_sum(0, 0, 2)
         pair_sum(0, 6)

@@ -25,7 +25,7 @@ HIDDEN_PASSES = H // K_PASS
 RAW_BYTES = PACK * K_PASS * 4
 W1_ON_VECTOR = 88
 W1B_ON_VECTOR = 76
-PLANE0_ON_SCALAR = 352
+PLANE0_ON_SCALAR = 320
 SCALAR_PIECES = ((0, 256), (256, 640), (640, 1024))
 
 
@@ -196,9 +196,9 @@ def tile_attend_mod_relu_kernel(tc, xT, w1, w2, offs, out):
         half_sum(0, 0, 2)
         pair_sum(0, 6)
         first_layer(hb[1], xb_mx, w1b_mx, {2: 2, 3: 6}, vector_relu)
-        half_sum(3, 0, 4)
+        half_sum(3, 0, 2)
         h_mx[1].append(quantized(hb[1], "hb1"))
-        pair_sum(1, 2)
+        pair_sum(1, 6)
         pair_sum(2, 5)
         pair_sum(3, 3)
         half_sum(0, 1, 7)

@@ -25,7 +25,7 @@ HIDDEN_PASSES = H // K_PASS
 RAW_BYTES = PACK * K_PASS * 4
 W1_ON_VECTOR = 88
 W1B_ON_VECTOR = 76
-PLANE0_ON_SCALAR = 320
+PLANE0_ON_SCALAR = 256
 SCALAR_PIECES = ((0, 256), (256, 640), (640, 1024))
 
 
@@ -140,6 +140,11 @@ def tile_attend_mod_relu_kernel(tc, xT, w1, w2, offs, out):
             product(bank[b][:], t, half, slice(0, HALF))
             nc.vector.tensor_tensor(totals[:, t, half * HALF : (half + 1) * HALF], bank[b][:], picked[:, half, t, :], ADD)
 
+        def quarter_sum(t, q, b):
+            cols = slice(q * QUARTER, (q + 1) * QUARTER)
+            product(bank[b][:, :QUARTER], t, 0, cols)
+            nc.vector.tensor_tensor(totals[:, t, cols], bank[b][:, :QUARTER], picked[:, 0, t, cols], ADD)
+
         def pair_sum(q, b):
             acc = bank[b][:].rearrange("p (k n) -> p k n", k=2)
             cols = slice(q % 2 * QUARTER, (q % 2 + 1) * QUARTER)
@@ -183,6 +188,7 @@ def tile_attend_mod_relu_kernel(tc, xT, w1, w2, offs, out):
         first_layer(joint[0][:, 0, :], xa_mx, w1a_mx, rotation)
         w1b_mx = quantized(w1b[:], "w1b")
         xb_mx = quantized(xb[:], "xb", 0)
+        first_layer(hb[1], xb_mx, w1b_mx, {2: 5}, vector_relu)
         first_layer(joint[1][:, 0, :], xa_mx, w1b_mx, rotation)
         first_layer(hb[0], xb_mx, w1a_mx, rotation)
         first_layer(hb[1], xb_mx, w1b_mx, {0: 0, 1: 1})
@@ -192,16 +198,17 @@ def tile_attend_mod_relu_kernel(tc, xT, w1, w2, offs, out):
         round_weight(nc.vector.tensor_copy, joint[1][:, 1, :], 0, P, w2_raw[1])
         h_mx[0].append(quantized(joint[1][:, 0, :], "ha1"))
         w2_mx.append(quantized(joint[1][:, 1, :], "w2b"))
+        quarter_sum(0, 0, 7)
         h_mx.append([quantized(hb[0], "hb0", 2 * RAW_BYTES + HIDDEN_PASSES * HALF * 4)])
-        half_sum(0, 0, 2)
+        quarter_sum(0, 1, 4)
         pair_sum(0, 6)
-        first_layer(hb[1], xb_mx, w1b_mx, {2: 2, 3: 6}, vector_relu)
-        half_sum(3, 0, 2)
+        first_layer(hb[1], xb_mx, w1b_mx, {3: 7}, vector_relu)
+        half_sum(3, 0, 6)
         h_mx[1].append(quantized(hb[1], "hb1"))
-        pair_sum(1, 6)
+        pair_sum(1, 7)
         pair_sum(2, 5)
         pair_sum(3, 3)
-        half_sum(0, 1, 7)
+        half_sum(0, 1, 4)
         half_sum(3, 1, 5)
         scatter(scalar_move, 0, 0, PLANE0_ON_SCALAR)
         for n0, n1 in SCALAR_PIECES:

@@ -25,7 +25,7 @@ HIDDEN_PASSES = H // K_PASS
 RAW_BYTES = PACK * K_PASS * 4
 W1_ON_VECTOR = 88
 W1B_ON_VECTOR = 76
-PLANE0_ON_SCALAR = 256
+PLANE0_ON_SCALAR = 288
 SCALAR_PIECES = ((0, 256), (256, 640), (640, 1024))
 
 
@@ -198,10 +198,10 @@ def tile_attend_mod_relu_kernel(tc, xT, w1, w2, offs, out):
         round_weight(nc.vector.tensor_copy, joint[1][:, 1, :], 0, P, w2_raw[1])
         h_mx[0].append(quantized(joint[1][:, 0, :], "ha1"))
         w2_mx.append(quantized(joint[1][:, 1, :], "w2b"))
-        quarter_sum(0, 0, 7)
+        quarter_sum(1, 0, 7)
         h_mx.append([quantized(hb[0], "hb0", 2 * RAW_BYTES + HIDDEN_PASSES * HALF * 4)])
-        quarter_sum(0, 1, 4)
-        pair_sum(0, 6)
+        half_sum(0, 0, 4)
+        quarter_sum(2, 0, 6)
         first_layer(hb[1], xb_mx, w1b_mx, {3: 7}, vector_relu)
         half_sum(3, 0, 6)
         h_mx[1].append(quantized(hb[1], "hb1"))
@@ -210,8 +210,10 @@ def tile_attend_mod_relu_kernel(tc, xT, w1, w2, offs, out):
         pair_sum(3, 3)
         half_sum(0, 1, 4)
         half_sum(3, 1, 5)
+        scatter(scalar_move, 1, *SCALAR_PIECES[0])
         scatter(scalar_move, 0, 0, PLANE0_ON_SCALAR)
-        for n0, n1 in SCALAR_PIECES:
+        scatter(scalar_move, 2, *SCALAR_PIECES[0])
+        for n0, n1 in SCALAR_PIECES[1:]:
             for t in (1, 2):
                 scatter(scalar_move, t, n0, n1)
         scatter(vector_move, 0, PLANE0_ON_SCALAR, G)

@@ -24,7 +24,6 @@ NB = 128
 HIDDEN_PASSES = H // K_PASS
 RAW_BYTES = PACK * K_PASS * 4
 W1_ON_VECTOR = 88
-W1B_ON_VECTOR = 76
 PLANE0_ON_SCALAR = 288
 SCALAR_PIECES = ((0, 256), (256, 640), (640, 1024))
 
@@ -47,9 +46,9 @@ def tile_attend_mod_relu_kernel(tc, xT, w1, w2, offs, out):
         out_rows = out.rearrange("(p t) c -> t p c", t=PACK)
         w1_rows = w1.rearrange("(p j) c -> p j c", j=PACK)
         planes = [sbuf([P, T], F32, f"plane{t}") for t in range(PACK)]
-        w1a_raw = sbuf([P, PACK, K_PASS], F32, "w1a_raw")
-        w1b_raw = sbuf([P, PACK, K_PASS], F32, "w1b_raw", 0)
-        w2_raw = [sbuf([P, PACK, D], F32, "w2_raw0"), sbuf([P, PACK, D], F32, "w2_raw1", 2 * RAW_BYTES)]
+        w1a_raw = sbuf([P, PACK, K_PASS], F32, "w1a_raw", 0)
+        w1b_raw = sbuf([P, PACK, K_PASS], F32, "w1b_raw")
+        w2_raw = [sbuf([P, PACK, D], F32, "w2_raw0", RAW_BYTES), sbuf([P, PACK, D], F32, "w2_raw1", 2 * RAW_BYTES)]
 
         nc.sync.dma_start(planes[0][:], x_rows[0])
         nc.sync.dma_start(offsets[:], offs)
@@ -179,21 +178,20 @@ def tile_attend_mod_relu_kernel(tc, xT, w1, w2, offs, out):
         round_weight(nc.scalar.copy, w1a[:], W1_ON_VECTOR, P, w1a_raw)
         round_weight(nc.vector.tensor_copy, w1a[:], 0, W1_ON_VECTOR, w1a_raw)
         w1a_mx = quantized(w1a[:], "w1a")
+        xb_mx = quantized(xb[:], "xb", 0)
         w1b = sbuf([P, K_PASS * PACK], BF16, "w1b")
-        round_weight(nc.scalar.copy, w1b[:], W1B_ON_VECTOR, P, w1b_raw)
-        round_weight(nc.vector.tensor_copy, w1b[:], 0, W1B_ON_VECTOR, w1b_raw)
-        joint = [sbuf([P, 2, HALF * PACK], BF16, "joint0", RAW_BYTES // 2), sbuf([P, 2, HALF * PACK], BF16, "joint1")]
+        round_weight(nc.vector.tensor_copy, w1b[:], 0, P, w1b_raw)
+        joint = [sbuf([P, 2, HALF * PACK], BF16, "joint0"), sbuf([P, 2, HALF * PACK], BF16, "joint1")]
         hb = [sbuf([P, HALF * PACK], BF16, f"hb{g}")[:] for g in range(HIDDEN_PASSES)]
         rotation = {b: b for b in range(HALF // NB)}
         first_layer(joint[0][:, 0, :], xa_mx, w1a_mx, rotation)
+        first_layer(hb[0], xb_mx, w1a_mx, {0: 0})
         w1b_mx = quantized(w1b[:], "w1b")
-        xb_mx = quantized(xb[:], "xb", 0)
-        first_layer(hb[1], xb_mx, w1b_mx, {2: 5}, vector_relu)
-        first_layer(joint[1][:, 0, :], xa_mx, w1b_mx, rotation)
-        first_layer(hb[0], xb_mx, w1a_mx, rotation)
-        first_layer(hb[1], xb_mx, w1b_mx, {0: 0, 1: 1})
+        first_layer(joint[1][:, 0, :], xa_mx, w1b_mx, {0: 1, 1: 2, 2: 3, 3: 0})
+        first_layer(hb[0], xb_mx, w1a_mx, {1: 1, 2: 2, 3: 3})
+        first_layer(hb[1], xb_mx, w1b_mx, {0: 0, 1: 1, 2: 2})
         round_weight(nc.vector.tensor_copy, joint[0][:, 1, :], 0, P, w2_raw[0])
-        h_mx = [[quantized(joint[0][:, 0, :], "ha0")]]
+        h_mx = [[quantized(joint[0][:, 0, :], "ha0", RAW_BYTES)]]
         w2_mx = [quantized(joint[0][:, 1, :], "w2a")]
         round_weight(nc.vector.tensor_copy, joint[1][:, 1, :], 0, P, w2_raw[1])
         h_mx[0].append(quantized(joint[1][:, 0, :], "ha1"))

@@ -23,7 +23,7 @@ QUARTER = 256
 NB = 128
 HIDDEN_PASSES = H // K_PASS
 RAW_BYTES = PACK * K_PASS * 4
-W1_ON_VECTOR = 88
+W1_ON_SCALAR = 40
 PLANE0_ON_SCALAR = 288
 SCALAR_PIECES = ((0, 256), (256, 640), (640, 1024))
 
@@ -46,8 +46,10 @@ def tile_attend_mod_relu_kernel(tc, xT, w1, w2, offs, out):
         out_rows = out.rearrange("(p t) c -> t p c", t=PACK)
         w1_rows = w1.rearrange("(p j) c -> p j c", j=PACK)
         planes = [sbuf([P, T], F32, f"plane{t}") for t in range(PACK)]
-        w1a_raw = sbuf([P, PACK, K_PASS], F32, "w1a_raw", 0)
-        w1b_raw = sbuf([P, PACK, K_PASS], F32, "w1b_raw")
+        shared = sbuf([P, PACK * G + PACK * K_PASS - QUARTER], F32, "shared")
+        picked = shared[:, : PACK * G].rearrange("p (h t n) -> p h t n", h=2, t=PACK)
+        w1a_raw = shared[:, PACK * G - QUARTER :].rearrange("p (j c) -> p j c", j=PACK)
+        w1b_raw = sbuf([P, PACK, K_PASS], F32, "w1b_raw", 0)
         w2_raw = [sbuf([P, PACK, D], F32, "w2_raw0", RAW_BYTES), sbuf([P, PACK, D], F32, "w2_raw1", 2 * RAW_BYTES)]
 
         nc.sync.dma_start(planes[0][:], x_rows[0])
@@ -65,17 +67,20 @@ def tile_attend_mod_relu_kernel(tc, xT, w1, w2, offs, out):
             src = raw[:].rearrange("p j (m i t) -> p m j i t", i=2, t=PACK)
             copy(dst[:, m0 // 2 : m1 // 2], src[:, (m0 - raw_m0) // 2 : (m1 - raw_m0) // 2])
 
+        def mx_tiles(width, label, tag=None):
+            return sbuf([P, width], U32, f"{label}_codes", tag), sbuf([P, width], U8, f"{label}_scales")
+
+        def quantize(mx, grouped, c0, c1):
+            nc.vector.quantize_mx(out=mx[0][:, c0:c1].bitcast(FP8X4), scales=mx[1][:, c0:c1], in_=grouped[:, c0 * PACK : c1 * PACK])
+
         def quantized(grouped, label, tag=None):
             width = grouped.shape[1] // PACK
-            codes = sbuf([P, width], U32, f"{label}_codes", tag)
-            scales = sbuf([P, width], U8, f"{label}_scales")
-            nc.vector.quantize_mx(out=codes[:].bitcast(FP8X4), scales=scales[:], in_=grouped)
-            return codes, scales
+            mx = mx_tiles(width, label, tag)
+            quantize(mx, grouped, 0, width)
+            return mx
 
         def by_pass(mx):
             return [(mx[0][:, g * HALF : (g + 1) * HALF], mx[1][:, g * HALF : (g + 1) * HALF]) for g in range(HIDDEN_PASSES)]
-
-        picked = sbuf([P, 2, PACK, HALF], F32, "picked")
 
         def listed(t, n0, n1):
             return planes[t][:].indirect(offsets[:, n0 // 16 : n1 // 16])
@@ -169,26 +174,28 @@ def tile_attend_mod_relu_kernel(tc, xT, w1, w2, offs, out):
         gather(vector_move, 3, 0, QUARTER)
         gather(scalar_move, 3, QUARTER, HALF)
         gather(scalar_move, 3, HALF, HALF + QUARTER)
-        gather(scalar_move, 3, HALF + QUARTER, G)
-        round_x(nc.vector.tensor_copy, xa[:], 0, 2, 4)
-        round_x(nc.vector.tensor_copy, xb[:], 1, 2, 4, 0, QUARTER)
-        round_x(nc.scalar.copy, xb[:], 1, 2, 4, QUARTER, HALF)
-        xa_mx = quantized(xa[:], "xa")
+        round_x(nc.vector.tensor_copy, xa[:], 0, 2, 4, 0, QUARTER)
+        round_x(nc.vector.tensor_copy, xa[:], 0, 2, 4, QUARTER, HALF)
+        round_x(nc.scalar.copy, xb[:], 1, 2, 4, 0, QUARTER)
+        xa_mx = mx_tiles(HALF, "xa")
+        quantize(xa_mx, xa[:], 0, QUARTER)
         w1a = sbuf([P, K_PASS * PACK], BF16, "w1a")
-        round_weight(nc.scalar.copy, w1a[:], W1_ON_VECTOR, P, w1a_raw)
-        round_weight(nc.vector.tensor_copy, w1a[:], 0, W1_ON_VECTOR, w1a_raw)
+        round_weight(nc.scalar.copy, w1a[:], 0, W1_ON_SCALAR, w1a_raw)
+        round_weight(nc.vector.tensor_copy, w1a[:], W1_ON_SCALAR, P, w1a_raw)
+        quantize(xa_mx, xa[:], QUARTER, HALF)
         w1a_mx = quantized(w1a[:], "w1a")
-        xb_mx = quantized(xb[:], "xb", 0)
+        gather(scalar_move, 3, HALF + QUARTER, G)
+        round_x(nc.scalar.copy, xb[:], 1, 2, 4, QUARTER, HALF)
         w1b = sbuf([P, K_PASS * PACK], BF16, "w1b")
         round_weight(nc.vector.tensor_copy, w1b[:], 0, P, w1b_raw)
         joint = [sbuf([P, 2, HALF * PACK], BF16, "joint0"), sbuf([P, 2, HALF * PACK], BF16, "joint1")]
         hb = [sbuf([P, HALF * PACK], BF16, f"hb{g}")[:] for g in range(HIDDEN_PASSES)]
         rotation = {b: b for b in range(HALF // NB)}
         first_layer(joint[0][:, 0, :], xa_mx, w1a_mx, rotation)
-        first_layer(hb[0], xb_mx, w1a_mx, {0: 0})
         w1b_mx = quantized(w1b[:], "w1b")
-        first_layer(joint[1][:, 0, :], xa_mx, w1b_mx, {0: 1, 1: 2, 2: 3, 3: 0})
-        first_layer(hb[0], xb_mx, w1a_mx, {1: 1, 2: 2, 3: 3})
+        xb_mx = quantized(xb[:], "xb", 0)
+        first_layer(joint[1][:, 0, :], xa_mx, w1b_mx, rotation)
+        first_layer(hb[0], xb_mx, w1a_mx, rotation)
         first_layer(hb[1], xb_mx, w1b_mx, {0: 0, 1: 1, 2: 2})
         round_weight(nc.vector.tensor_copy, joint[0][:, 1, :], 0, P, w2_raw[0])
         h_mx = [[quantized(joint[0][:, 0, :], "ha0", RAW_BYTES)]]

@@ -24,7 +24,7 @@ NB = 128
 HIDDEN_PASSES = H // K_PASS
 RAW_BYTES = PACK * K_PASS * 4
 W1_ON_SCALAR = 40
-PLANE0_ON_SCALAR = 288
+PLANE2_ON_SCALAR = 256
 SCALAR_PIECES = ((0, 256), (256, 640), (640, 1024))
 
 
@@ -50,7 +50,8 @@ def tile_attend_mod_relu_kernel(tc, xT, w1, w2, offs, out):
         picked = shared[:, : PACK * G].rearrange("p (h t n) -> p h t n", h=2, t=PACK)
         w1a_raw = shared[:, PACK * G - QUARTER :].rearrange("p (j c) -> p j c", j=PACK)
         w1b_raw = sbuf([P, PACK, K_PASS], F32, "w1b_raw", 0)
-        w2_raw = [sbuf([P, PACK, D], F32, "w2_raw0", RAW_BYTES), sbuf([P, PACK, D], F32, "w2_raw1", 2 * RAW_BYTES)]
+        late = sbuf([P, 3 * QUARTER + PACK * D], F32, "late", 2 * RAW_BYTES)
+        w2_raw = [sbuf([P, PACK, D], F32, "w2_raw0", RAW_BYTES)[:], late[:, 3 * QUARTER :].rearrange("p (j c) -> p j c", j=PACK)]
 
         nc.sync.dma_start(planes[0][:], x_rows[0])
         nc.sync.dma_start(offsets[:], offs)
@@ -60,7 +61,7 @@ def tile_attend_mod_relu_kernel(tc, xT, w1, w2, offs, out):
         nc.sync.dma_start(w1b_raw[:], w1_rows[:, :, K_PASS:])
         for g in range(HIDDEN_PASSES):
             rows = w2[g * K_PASS : (g + 1) * K_PASS, :].rearrange("(p j) c -> p j c", j=PACK)
-            nc.sync.dma_start(w2_raw[g][:], rows)
+            nc.sync.dma_start(w2_raw[g], rows)
 
         def round_weight(copy, grouped, m0, m1, raw, raw_m0=0):
             dst = grouped.rearrange("p (t m i j) -> p m j i t", t=PACK, i=2, j=PACK)
@@ -78,9 +79,6 @@ def tile_attend_mod_relu_kernel(tc, xT, w1, w2, offs, out):
             mx = mx_tiles(width, label, tag)
             quantize(mx, grouped, 0, width)
             return mx
-
-        def by_pass(mx):
-            return [(mx[0][:, g * HALF : (g + 1) * HALF], mx[1][:, g * HALF : (g + 1) * HALF]) for g in range(HIDDEN_PASSES)]
 
         def listed(t, n0, n1):
             return planes[t][:].indirect(offsets[:, n0 // 16 : n1 // 16])
@@ -106,37 +104,40 @@ def tile_attend_mod_relu_kernel(tc, xT, w1, w2, offs, out):
         def vector_relu(dst, src):
             nc.vector.tensor_scalar_max(dst, src, 0.0)
 
-        def first_layer(hidden, x_mx, w_mx, banks, relu=scalar_relu):
-            dst = hidden.rearrange("p (n t) -> p n t", t=PACK)
-            for b in banks:
-                cols = slice(b * NB, (b + 1) * NB)
-                acc = bank[banks[b]][:].rearrange("p (t n) -> p t n", t=PACK)
-                for t in range(PACK):
-                    chans = slice(t * P, (t + 1) * P)
-                    nc.tensor.matmul_mx(
-                        out=acc[:, t, :],
-                        lhsT=w_mx[0][:, chans].bitcast(FP8X4),
-                        lhsT_scale=w_mx[1][:, chans],
-                        rhs=x_mx[0][:, cols].bitcast(FP8X4),
-                        rhs_scale=x_mx[1][:, cols],
-                        start=True,
-                        stop=True,
-                    )
-                relu(dst[:, cols, :], acc.rearrange("p t n -> p n t"))
+        def hidden_block(g, block, b, relu=scalar_relu):
+            half, within = divmod(block, HALF // NB)
+            dst = h_bf[half, g].rearrange("p (n t) -> p n t", t=PACK)
+            codes, scales = x_blocks[block]
+            acc = bank[b][:].rearrange("p (t n) -> p t n", t=PACK)
+            for t in range(PACK):
+                chans = slice(t * P, (t + 1) * P)
+                nc.tensor.matmul_mx(
+                    out=acc[:, t, :],
+                    lhsT=w1_mx[g][0][:, chans].bitcast(FP8X4),
+                    lhsT_scale=w1_mx[g][1][:, chans],
+                    rhs=codes.bitcast(FP8X4),
+                    rhs_scale=scales,
+                    start=True,
+                    stop=True,
+                )
+            relu(dst[:, within * NB : (within + 1) * NB, :], acc.rearrange("p t n -> p n t"))
+
+        def one_pass(acc, t, half, cols, g, start, stop):
+            chans = slice(t * P, (t + 1) * P)
+            codes, scales = h_mx[half, g]
+            nc.tensor.matmul_mx(
+                out=acc,
+                lhsT=w2_mx[g][0][:, chans].bitcast(FP8X4),
+                lhsT_scale=w2_mx[g][1][:, chans],
+                rhs=codes[:, cols].bitcast(FP8X4),
+                rhs_scale=scales[:, cols],
+                start=start,
+                stop=stop,
+            )
 
         def product(acc, t, half, cols):
             for g in range(HIDDEN_PASSES):
-                chans = slice(t * P, (t + 1) * P)
-                codes, scales = h_mx[half][g]
-                nc.tensor.matmul_mx(
-                    out=acc,
-                    lhsT=w2_mx[g][0][:, chans].bitcast(FP8X4),
-                    lhsT_scale=w2_mx[g][1][:, chans],
-                    rhs=codes[:, cols].bitcast(FP8X4),
-                    rhs_scale=scales[:, cols],
-                    start=(g == 0),
-                    stop=(g == HIDDEN_PASSES - 1),
-                )
+                one_pass(acc, t, half, cols, g, g == 0, g == HIDDEN_PASSES - 1)
 
         totals = sbuf([P, PACK, G], F32, "totals")
 
@@ -144,17 +145,18 @@ def tile_attend_mod_relu_kernel(tc, xT, w1, w2, offs, out):
             product(bank[b][:], t, half, slice(0, HALF))
             nc.vector.tensor_tensor(totals[:, t, half * HALF : (half + 1) * HALF], bank[b][:], picked[:, half, t, :], ADD)
 
-        def quarter_sum(t, q, b):
-            cols = slice(q * QUARTER, (q + 1) * QUARTER)
-            product(bank[b][:, :QUARTER], t, 0, cols)
-            nc.vector.tensor_tensor(totals[:, t, cols], bank[b][:, :QUARTER], picked[:, 0, t, cols], ADD)
+        def quarter_sum(t, b):
+            cols = slice(0, QUARTER)
+            product(bank[b][:, cols], t, 0, cols)
+            nc.vector.tensor_tensor(totals[:, t, cols], bank[b][:, cols], picked[:, 0, t, cols], ADD)
 
         def pair_sum(q, b):
             acc = bank[b][:].rearrange("p (k n) -> p k n", k=2)
             cols = slice(q % 2 * QUARTER, (q % 2 + 1) * QUARTER)
-            for k in range(2):
-                product(acc[:, k, :], 1 + k, q // 2, cols)
-            nc.vector.tensor_tensor(totals[:, 1:3, q * QUARTER : (q + 1) * QUARTER], acc, picked[:, q // 2, 1:3, cols], ADD)
+            for g in range(HIDDEN_PASSES):
+                for k in range(2):
+                    one_pass(acc[:, k, :], k, q // 2, cols, g, g == 0 and k == 0, g == HIDDEN_PASSES - 1 and k == 1)
+            nc.vector.tensor_tensor(totals[:, 0:2, q * QUARTER : (q + 1) * QUARTER], acc, picked[:, q // 2, 0:2, cols], ADD)
 
         def scatter(move, t, n0, n1):
             move(listed(t, n0, n1), totals[:, t, n0:n1])
@@ -188,40 +190,40 @@ def tile_attend_mod_relu_kernel(tc, xT, w1, w2, offs, out):
         round_x(nc.scalar.copy, xb[:], 1, 2, 4, QUARTER, HALF)
         w1b = sbuf([P, K_PASS * PACK], BF16, "w1b")
         round_weight(nc.vector.tensor_copy, w1b[:], 0, P, w1b_raw)
-        joint = [sbuf([P, 2, HALF * PACK], BF16, "joint0"), sbuf([P, 2, HALF * PACK], BF16, "joint1")]
-        hb = [sbuf([P, HALF * PACK], BF16, f"hb{g}")[:] for g in range(HIDDEN_PASSES)]
-        rotation = {b: b for b in range(HALF // NB)}
-        first_layer(joint[0][:, 0, :], xa_mx, w1a_mx, rotation)
-        w1b_mx = quantized(w1b[:], "w1b")
+        w1_mx = [w1a_mx, quantized(w1b[:], "w1b")]
         xb_mx = quantized(xb[:], "xb", 0)
-        first_layer(joint[1][:, 0, :], xa_mx, w1b_mx, rotation)
-        first_layer(hb[0], xb_mx, w1a_mx, rotation)
-        first_layer(hb[1], xb_mx, w1b_mx, {0: 0, 1: 1, 2: 2})
-        round_weight(nc.vector.tensor_copy, joint[0][:, 1, :], 0, P, w2_raw[0])
-        h_mx = [[quantized(joint[0][:, 0, :], "ha0", RAW_BYTES)]]
-        w2_mx = [quantized(joint[0][:, 1, :], "w2a")]
-        round_weight(nc.vector.tensor_copy, joint[1][:, 1, :], 0, P, w2_raw[1])
-        h_mx[0].append(quantized(joint[1][:, 0, :], "ha1"))
-        w2_mx.append(quantized(joint[1][:, 1, :], "w2b"))
-        quarter_sum(1, 0, 7)
-        h_mx.append([quantized(hb[0], "hb0", 2 * RAW_BYTES + HIDDEN_PASSES * HALF * 4)])
-        half_sum(0, 0, 4)
-        quarter_sum(2, 0, 6)
-        first_layer(hb[1], xb_mx, w1b_mx, {3: 7}, vector_relu)
-        half_sum(3, 0, 6)
-        h_mx[1].append(quantized(hb[1], "hb1"))
-        pair_sum(1, 7)
+        x_blocks = [(codes[:, c : c + NB], scales[:, c : c + NB]) for codes, scales in (xa_mx, xb_mx) for c in range(0, codes.shape[1], NB)]
+        h_bf = {(0, g): sbuf([P, HALF * PACK], BF16, f"ha{g}")[:] for g in range(HIDDEN_PASSES)}
+        h_bf[1, 0] = late[:, : PACK * QUARTER].bitcast(BF16)
+        h_bf[1, 1] = sbuf([P, HALF * PACK], BF16, "hb1")[:]
+        w2_bf = [sbuf([P, D * PACK], BF16, f"w2_bf{g}")[:] for g in range(HIDDEN_PASSES)]
+        h_mx, w2_mx = {}, {}
+        rows = ((0, range(0, 4)), (1, range(0, 4)), (0, range(4, 7)), (1, range(4, 8)))
+        for n, (g, block) in enumerate((g, block) for g, blocks in rows for block in blocks):
+            hidden_block(g, block, n % 4)
+        for g in range(HIDDEN_PASSES):
+            round_weight(nc.vector.tensor_copy, w2_bf[g], 0, P, w2_raw[g])
+            h_mx[0, g] = quantized(h_bf[0, g], f"ha{g}", RAW_BYTES if g == 0 else None)
+            w2_mx[g] = quantized(w2_bf[g], f"w2_{g}")
+        hidden_block(0, 7, 7, vector_relu)
+        quarter_sum(0, 4)
+        h_mx[1, 0] = quantized(h_bf[1, 0], "hb0")
+        half_sum(2, 0, 5)
+        quarter_sum(1, 6)
+        h_mx[1, 1] = quantized(h_bf[1, 1], "hb1", 2 * RAW_BYTES)
+        half_sum(3, 0, 7)
+        pair_sum(1, 4)
         pair_sum(2, 5)
-        pair_sum(3, 3)
-        half_sum(0, 1, 4)
-        half_sum(3, 1, 5)
+        pair_sum(3, 6)
+        half_sum(2, 1, 7)
+        half_sum(3, 1, 4)
+        scatter(scalar_move, 0, *SCALAR_PIECES[0])
+        scatter(scalar_move, 2, 0, PLANE2_ON_SCALAR)
         scatter(scalar_move, 1, *SCALAR_PIECES[0])
-        scatter(scalar_move, 0, 0, PLANE0_ON_SCALAR)
-        scatter(scalar_move, 2, *SCALAR_PIECES[0])
         for n0, n1 in SCALAR_PIECES[1:]:
-            for t in (1, 2):
+            for t in (0, 1):
                 scatter(scalar_move, t, n0, n1)
-        scatter(vector_move, 0, PLANE0_ON_SCALAR, G)
+        scatter(vector_move, 2, PLANE2_ON_SCALAR, G)
         scatter(vector_move, 3, 0, G)
-        for t, queue in enumerate((nc.sync, nc.scalar, nc.scalar, nc.sync)):
+        for t, queue in ((2, nc.sync), (0, nc.scalar), (1, nc.scalar), (3, nc.sync)):
             queue.dma_start(out_rows[t], planes[t][:])

@@ -106,7 +106,7 @@ def tile_attend_mod_relu_kernel(tc, xT, w1, w2, offs, out):
 
         def hidden_block(g, block, b, relu=scalar_relu):
             half, within = divmod(block, HALF // NB)
-            dst = h_bf[half, g].rearrange("p (n t) -> p n t", t=PACK)
+            dst = h_bf[half, g].rearrange("p (n e t) -> p n t e", e=2, t=PACK)
             codes, scales = x_blocks[block]
             acc = bank[b][:].rearrange("p (t n) -> p t n", t=PACK)
             for t in range(PACK):
@@ -120,7 +120,7 @@ def tile_attend_mod_relu_kernel(tc, xT, w1, w2, offs, out):
                     start=True,
                     stop=True,
                 )
-            relu(dst[:, within * NB : (within + 1) * NB, :], acc.rearrange("p t n -> p n t"))
+            relu(dst[:, within * NB // 2 : (within + 1) * NB // 2], acc.rearrange("p t (n e) -> p n t e", e=2))
 
         def one_pass(acc, t, half, cols, g, start, stop):
             chans = slice(t * P, (t + 1) * P)

@@ -23,6 +23,7 @@ QUARTER = 256
 NB = 128
 HIDDEN_PASSES = H // K_PASS
 RAW_BYTES = PACK * K_PASS * 4
+XA_AT = 3 * RAW_BYTES + 3 * QUARTER * 4
 W1_ON_SCALAR = 40
 PLANE2_ON_SCALAR = 256
 SCALAR_PIECES = ((0, 256), (256, 640), (640, 1024))
@@ -179,32 +180,40 @@ def tile_attend_mod_relu_kernel(tc, xT, w1, w2, offs, out):
         round_x(nc.vector.tensor_copy, xa[:], 0, 2, 4, 0, QUARTER)
         round_x(nc.vector.tensor_copy, xa[:], 0, 2, 4, QUARTER, HALF)
         round_x(nc.scalar.copy, xb[:], 1, 2, 4, 0, QUARTER)
-        xa_mx = mx_tiles(HALF, "xa")
-        quantize(xa_mx, xa[:], 0, QUARTER)
+        xa_mx = [quantized(xa[:, : QUARTER * PACK], "xa0", XA_AT)]
         w1a = sbuf([P, K_PASS * PACK], BF16, "w1a")
         round_weight(nc.scalar.copy, w1a[:], 0, W1_ON_SCALAR, w1a_raw)
         round_weight(nc.vector.tensor_copy, w1a[:], W1_ON_SCALAR, P, w1a_raw)
-        quantize(xa_mx, xa[:], QUARTER, HALF)
+        xa_mx.append(quantized(xa[:, QUARTER * PACK :], "xa1"))
         w1a_mx = quantized(w1a[:], "w1a")
         gather(scalar_move, 3, HALF + QUARTER, G)
         round_x(nc.scalar.copy, xb[:], 1, 2, 4, QUARTER, HALF)
         w1b = sbuf([P, K_PASS * PACK], BF16, "w1b")
         round_weight(nc.vector.tensor_copy, w1b[:], 0, P, w1b_raw)
         w1_mx = [w1a_mx, quantized(w1b[:], "w1b")]
-        xb_mx = quantized(xb[:], "xb", 0)
-        x_blocks = [(codes[:, c : c + NB], scales[:, c : c + NB]) for codes, scales in (xa_mx, xb_mx) for c in range(0, codes.shape[1], NB)]
-        h_bf = {(0, g): sbuf([P, HALF * PACK], BF16, f"ha{g}")[:] for g in range(HIDDEN_PASSES)}
+        xb_mx = quantized(xb[:, : QUARTER * PACK], "xb", 0)
+        xc_mx = mx_tiles(QUARTER, "xc", XA_AT)
+        x_blocks = [(codes[:, c : c + NB], scales[:, c : c + NB]) for codes, scales in (*xa_mx, xb_mx, xc_mx) for c in range(0, codes.shape[1], NB)]
+        joint = sbuf([P, 2, HALF * PACK], BF16, "joint")
+        h_bf = {(0, 0): joint[:, 0, :], (0, 1): sbuf([P, HALF * PACK], BF16, "ha1")[:]}
         h_bf[1, 0] = late[:, : PACK * QUARTER].bitcast(BF16)
         h_bf[1, 1] = sbuf([P, HALF * PACK], BF16, "hb1")[:]
-        w2_bf = [sbuf([P, D * PACK], BF16, f"w2_bf{g}")[:] for g in range(HIDDEN_PASSES)]
+        w2_bf = [joint[:, 1, :], sbuf([P, D * PACK], BF16, "w2_bf1")[:]]
         h_mx, w2_mx = {}, {}
-        rows = ((0, range(0, 4)), (1, range(0, 4)), (0, range(4, 7)), (1, range(4, 8)))
-        for n, (g, block) in enumerate((g, block) for g, blocks in rows for block in blocks):
+        early_blocks = [(g, block) for g in range(HIDDEN_PASSES) for block in range(4)]
+        late_blocks = [(0, 4), (0, 5), (0, 6), (1, 4), (1, 5), (1, 6), (1, 7)]
+        for n, (g, block) in enumerate(early_blocks):
             hidden_block(g, block, n % 4)
-        for g in range(HIDDEN_PASSES):
-            round_weight(nc.vector.tensor_copy, w2_bf[g], 0, P, w2_raw[g])
-            h_mx[0, g] = quantized(h_bf[0, g], f"ha{g}", RAW_BYTES if g == 0 else None)
-            w2_mx[g] = quantized(w2_bf[g], f"w2_{g}")
+        round_weight(nc.vector.tensor_copy, w2_bf[0], 0, P, w2_raw[0])
+        quantize(xc_mx, xb[:, QUARTER * PACK :], 0, QUARTER)
+        codes, scales = quantized(joint[:].rearrange("p k n -> p (k n)"), "joint", RAW_BYTES)
+        h_mx[0, 0] = (codes[:, :HALF], scales[:, :HALF])
+        w2_mx[0] = (codes[:, HALF:], scales[:, HALF:])
+        for n, (g, block) in enumerate(late_blocks, len(early_blocks)):
+            hidden_block(g, block, n % 4)
+        round_weight(nc.vector.tensor_copy, w2_bf[1], 0, P, w2_raw[1])
+        h_mx[0, 1] = quantized(h_bf[0, 1], "ha1")
+        w2_mx[1] = quantized(w2_bf[1], "w2_1")
         hidden_block(0, 7, 7, vector_relu)
         quarter_sum(0, 4)
         h_mx[1, 0] = quantized(h_bf[1, 0], "hb0")

from contextlib import ExitStack

import concourse.mybir as mybir

D, T, G, H = 512, 2048, 1024, 1024
FLOPS = 2 * 2 * D * H * G

F32 = mybir.dt.float32
BF16 = mybir.dt.bfloat16
U32 = mybir.dt.uint32
U16 = mybir.dt.uint16
U8 = mybir.dt.uint8
FP8X4 = mybir.dt.float8_e4m3fn_x4
RELU = mybir.ActivationFunctionType.Relu
COPY = mybir.ActivationFunctionType.Copy
ADD = mybir.AluOpType.add

P = 128
PACK = 4
K_PASS = P * PACK
HALF = 512
QUARTER = 256
NB = 128
HIDDEN_PASSES = H // K_PASS
RAW_BYTES = PACK * K_PASS * 4
XA_AT = 3 * RAW_BYTES + 3 * QUARTER * 4
W1_ON_SCALAR = 40
PLANE2_ON_SCALAR = 256
SCALAR_PIECES = ((0, 256), (256, 640), (640, 1024))


def tile_attend_mod_relu_kernel(tc, xT, w1, w2, offs, out):
    nc = tc.nc
    with ExitStack() as ctx:
        keep = ctx.enter_context(tc.tile_pool(name="keep", bufs=1))
        reused = ctx.enter_context(tc.tile_pool(name="reused", bufs=1))
        psum = ctx.enter_context(tc.psum_pool(name="psum", bufs=1))

        def sbuf(shape, dtype, label, tag=None):
            if isinstance(tag, int):
                return reused.tile(shape, dtype, align_bytes=64, offset=tag, name=label)
            return keep.tile(shape, dtype, align_bytes=64, tag=tag or label, name=label)

        bank = [psum.tile([P, HALF], F32, name=f"bank{b}") for b in range(8)]
        offsets = keep.tile([P, G // 16], U16, name="offsets")
        x_rows = xT.rearrange("(p t) c -> t p c", t=PACK)
        out_rows = out.rearrange("(p t) c -> t p c", t=PACK)
        w1_rows = w1.rearrange("(p j) c -> p j c", j=PACK)
        planes = [sbuf([P, T], F32, f"plane{t}") for t in range(PACK)]
        shared = sbuf([P, PACK * G + PACK * K_PASS - QUARTER], F32, "shared")
        picked = shared[:, : PACK * G].rearrange("p (h t n) -> p h t n", h=2, t=PACK)
        w1a_raw = shared[:, PACK * G - QUARTER :].rearrange("p (j c) -> p j c", j=PACK)
        w1b_raw = sbuf([P, PACK, K_PASS], F32, "w1b_raw", 0)
        late = sbuf([P, 3 * QUARTER + PACK * D], F32, "late", 2 * RAW_BYTES)
        w2_raw = [sbuf([P, PACK, D], F32, "w2_raw0", RAW_BYTES)[:], late[:, 3 * QUARTER :].rearrange("p (j c) -> p j c", j=PACK)]

        nc.sync.dma_start(planes[0][:], x_rows[0])
        nc.sync.dma_start(offsets[:], offs)
        for t in range(1, PACK):
            nc.sync.dma_start(planes[t][:], x_rows[t])
        nc.sync.dma_start(w1a_raw[:], w1_rows[:, :, :K_PASS])
        nc.sync.dma_start(w1b_raw[:], w1_rows[:, :, K_PASS:])
        for g in range(HIDDEN_PASSES):
            rows = w2[g * K_PASS : (g + 1) * K_PASS, :].rearrange("(p j) c -> p j c", j=PACK)
            nc.sync.dma_start(w2_raw[g], rows)

        def round_weight(copy, grouped, m0, m1, raw, raw_m0=0):
            dst = grouped.rearrange("p (t m i j) -> p m j i t", t=PACK, i=2, j=PACK)
            src = raw[:].rearrange("p j (m i t) -> p m j i t", i=2, t=PACK)
            copy(dst[:, m0 // 2 : m1 // 2], src[:, (m0 - raw_m0) // 2 : (m1 - raw_m0) // 2])

        def mx_tiles(width, label, tag=None):
            return sbuf([P, width], U32, f"{label}_codes", tag), sbuf([P, width], U8, f"{label}_scales")

        def quantize(mx, grouped, c0, c1):
            nc.vector.quantize_mx(out=mx[0][:, c0:c1].bitcast(FP8X4), scales=mx[1][:, c0:c1], in_=grouped[:, c0 * PACK : c1 * PACK])

        def quantized(grouped, label, tag=None):
            width = grouped.shape[1] // PACK
            mx = mx_tiles(width, label, tag)
            quantize(mx, grouped, 0, width)
            return mx

        def listed(t, n0, n1):
            return planes[t][:].indirect(offsets[:, n0 // 16 : n1 // 16])

        def vector_move(dst, src):
            nc.vector.tensor_copy(dst, src)

        def scalar_move(dst, src):
            nc.scalar.activation(dst, src, COPY)

        def gather(move, t, n0, n1):
            half = n0 // HALF
            move(picked[:, half, t, n0 - half * HALF : n1 - half * HALF], listed(t, n0, n1))

        def round_x(copy, grouped, half, t0, t1, n0=0, n1=HALF):
            dst = grouped[:, n0 * PACK : n1 * PACK].rearrange("p (c i t) -> p c t i", i=PACK, t=PACK)
            src = picked[:, half, t0:t1, n0:n1].rearrange("p t (c i) -> p c t i", i=PACK)
            copy(dst[:, :, t0:t1], src)

        def scalar_relu(dst, src):
            nc.scalar.activation(dst, src, RELU)

        def vector_relu(dst, src):
            nc.vector.tensor_scalar_max(dst, src, 0.0)

        def hidden_block(g, block, b, relu=scalar_relu):
            half, within = divmod(block, HALF // NB)
            dst = h_bf[half, g].rearrange("p (n e t) -> p n t e", e=2, t=PACK)
            codes, scales = x_blocks[block]
            acc = bank[b][:].rearrange("p (t n) -> p t n", t=PACK)
            for t in range(PACK):
                chans = slice(t * P, (t + 1) * P)
                nc.tensor.matmul_mx(
                    out=acc[:, t, :],
                    lhsT=w1_mx[g][0][:, chans].bitcast(FP8X4),
                    lhsT_scale=w1_mx[g][1][:, chans],
                    rhs=codes.bitcast(FP8X4),
                    rhs_scale=scales,
                    start=True,
                    stop=True,
                )
            relu(dst[:, within * NB // 2 : (within + 1) * NB // 2], acc.rearrange("p t (n e) -> p n t e", e=2))

        def one_pass(acc, t, half, cols, g, start, stop):
            chans = slice(t * P, (t + 1) * P)
            codes, scales = h_mx[half, g]
            nc.tensor.matmul_mx(
                out=acc,
                lhsT=w2_mx[g][0][:, chans].bitcast(FP8X4),
                lhsT_scale=w2_mx[g][1][:, chans],
                rhs=codes[:, cols].bitcast(FP8X4),
                rhs_scale=scales[:, cols],
                start=start,
                stop=stop,
            )

        def product(acc, t, half, cols):
            for g in range(HIDDEN_PASSES):
                one_pass(acc, t, half, cols, g, g == 0, g == HIDDEN_PASSES - 1)

        totals = sbuf([P, PACK, G], F32, "totals")

        def half_sum(t, half, b):
            product(bank[b][:], t, half, slice(0, HALF))
            nc.vector.tensor_tensor(totals[:, t, half * HALF : (half + 1) * HALF], bank[b][:], picked[:, half, t, :], ADD)

        def quarter_sum(t, b):
            cols = slice(0, QUARTER)
            product(bank[b][:, cols], t, 0, cols)
            nc.vector.tensor_tensor(totals[:, t, cols], bank[b][:, cols], picked[:, 0, t, cols], ADD)

        def pair_sum(q, b):
            acc = bank[b][:].rearrange("p (k n) -> p k n", k=2)
            cols = slice(q % 2 * QUARTER, (q % 2 + 1) * QUARTER)
            for g in range(HIDDEN_PASSES):
                for k in range(2):
                    one_pass(acc[:, k, :], k, q // 2, cols, g, g == 0 and k == 0, g == HIDDEN_PASSES - 1 and k == 1)
            nc.vector.tensor_tensor(totals[:, 0:2, q * QUARTER : (q + 1) * QUARTER], acc, picked[:, q // 2, 0:2, cols], ADD)

        def scatter(move, t, n0, n1):
            move(listed(t, n0, n1), totals[:, t, n0:n1])

        xa = sbuf([P, HALF * PACK], BF16, "xa")
        xb = sbuf([P, HALF * PACK], BF16, "xb")
        gather(vector_move, 0, 0, HALF)
        round_x(nc.scalar.copy, xa[:], 0, 0, 1, 0, QUARTER)
        gather(vector_move, 0, HALF, G)
        gather(vector_move, 1, 0, HALF)
        gather(scalar_move, 1, HALF, G)
        round_x(nc.scalar.copy, xa[:], 0, 1, 2, 0, QUARTER)
        round_x(nc.vector.tensor_copy, xa[:], 0, 0, 2, QUARTER, HALF)
        round_x(nc.vector.tensor_copy, xb[:], 1, 0, 2)
        gather(vector_move, 2, 0, HALF)
        gather(scalar_move, 2, HALF, G)
        gather(vector_move, 3, 0, QUARTER)
        gather(scalar_move, 3, QUARTER, HALF)
        gather(scalar_move, 3, HALF, HALF + QUARTER)
        round_x(nc.vector.tensor_copy, xa[:], 0, 2, 4, 0, QUARTER)
        round_x(nc.vector.tensor_copy, xa[:], 0, 2, 4, QUARTER, HALF)
        round_x(nc.scalar.copy, xb[:], 1, 2, 4, 0, QUARTER)
        xa_mx = [quantized(xa[:, : QUARTER * PACK], "xa0", XA_AT)]
        w1a = sbuf([P, K_PASS * PACK], BF16, "w1a")
        round_weight(nc.scalar.copy, w1a[:], 0, W1_ON_SCALAR, w1a_raw)
        round_weight(nc.vector.tensor_copy, w1a[:], W1_ON_SCALAR, P, w1a_raw)
        xa_mx.append(quantized(xa[:, QUARTER * PACK :], "xa1"))
        w1a_mx = quantized(w1a[:], "w1a")
        gather(scalar_move, 3, HALF + QUARTER, G)
        round_x(nc.scalar.copy, xb[:], 1, 2, 4, QUARTER, HALF)
        w1b = sbuf([P, K_PASS * PACK], BF16, "w1b")
        round_weight(nc.vector.tensor_copy, w1b[:], 0, P, w1b_raw)
        w1_mx = [w1a_mx, quantized(w1b[:], "w1b")]
        xb_mx = quantized(xb[:, : QUARTER * PACK], "xb", 0)
        xc_mx = mx_tiles(QUARTER, "xc", XA_AT)
        x_blocks = [(codes[:, c : c + NB], scales[:, c : c + NB]) for codes, scales in (*xa_mx, xb_mx, xc_mx) for c in range(0, codes.shape[1], NB)]
        joint = sbuf([P, 2, HALF * PACK], BF16, "joint")
        h_bf = {(0, 0): joint[:, 0, :], (0, 1): sbuf([P, HALF * PACK], BF16, "ha1")[:]}
        h_bf[1, 0] = late[:, : PACK * QUARTER].bitcast(BF16)
        h_bf[1, 1] = sbuf([P, HALF * PACK], BF16, "hb1")[:]
        w2_bf = [joint[:, 1, :], sbuf([P, D * PACK], BF16, "w2_bf1")[:]]
        h_mx, w2_mx = {}, {}
        early_blocks = [(g, block) for g in range(HIDDEN_PASSES) for block in range(4)]
        late_blocks = [(0, 4), (0, 5), (0, 6), (1, 4), (1, 5), (1, 6), (1, 7)]
        for n, (g, block) in enumerate(early_blocks):
            hidden_block(g, block, n % 4)
        round_weight(nc.vector.tensor_copy, w2_bf[0], 0, P, w2_raw[0])
        quantize(xc_mx, xb[:, QUARTER * PACK :], 0, QUARTER)
        codes, scales = quantized(joint[:].rearrange("p k n -> p (k n)"), "joint", RAW_BYTES)
        h_mx[0, 0] = (codes[:, :HALF], scales[:, :HALF])
        w2_mx[0] = (codes[:, HALF:], scales[:, HALF:])
        for n, (g, block) in enumerate(late_blocks, len(early_blocks)):
            hidden_block(g, block, n % 4)
        round_weight(nc.vector.tensor_copy, w2_bf[1], 0, P, w2_raw[1])
        h_mx[0, 1] = quantized(h_bf[0, 1], "ha1")
        w2_mx[1] = quantized(w2_bf[1], "w2_1")
        hidden_block(0, 7, 7, vector_relu)
        quarter_sum(0, 4)
        h_mx[1, 0] = quantized(h_bf[1, 0], "hb0")
        half_sum(2, 0, 5)
        quarter_sum(1, 6)
        h_mx[1, 1] = quantized(h_bf[1, 1], "hb1", 2 * RAW_BYTES)
        half_sum(3, 0, 7)
        pair_sum(1, 4)
        pair_sum(2, 5)
        pair_sum(3, 6)
        half_sum(2, 1, 7)
        half_sum(3, 1, 4)
        scatter(scalar_move, 0, *SCALAR_PIECES[0])
        scatter(scalar_move, 2, 0, PLANE2_ON_SCALAR)
        scatter(scalar_move, 1, *SCALAR_PIECES[0])
        for n0, n1 in SCALAR_PIECES[1:]:
            for t in (0, 1):
                scatter(scalar_move, t, n0, n1)
        scatter(vector_move, 2, PLANE2_ON_SCALAR, G)
        scatter(vector_move, 3, 0, G)
        for t, queue in ((2, nc.sync), (0, nc.scalar), (1, nc.scalar), (3, nc.sync)):
            queue.dma_start(out_rows[t], planes[t][:])
